import numpy as np
import ml_dtypes


def mxq(x, axis, fmt="e4m3"):
    dtype, down = {"e4m3": (ml_dtypes.float8_e4m3fn, 7), "e5m2": (ml_dtypes.float8_e5m2, 14)}[fmt]
    v = np.moveaxis(np.asarray(x, np.float32).astype(ml_dtypes.bfloat16).astype(np.float64), axis, -1)
    blocks = v.reshape(v.shape[:-1] + (-1, 32))
    amax = np.abs(blocks).max(-1, keepdims=True)
    byte = np.maximum(np.where(amax > 0, np.frexp(amax)[1] - 1 + 127, 0) - down, 1)
    scale = np.exp2(byte - 127.0)
    codes = (blocks / scale).astype(np.float32).astype(dtype).astype(np.float64)
    return np.moveaxis((codes * scale).reshape(v.shape), -1, axis)


WIDE = False


def mx_kscale(k):
    if not WIDE:
        return np.ones(k)
    levels = np.array([24, -24, 12, -12, 0])
    if k % 512:
        return np.exp2(np.random.permutation(np.resize(levels, k // 32))).repeat(32)
    a = np.empty((k // 512, 16))
    for p in range(k // 512):
        a[p, :8] = np.random.permutation(np.resize(levels, 8))
        for g in range(8):
            far = levels[np.abs(levels - a[p, g]) >= 10]
            a[p, g + 8] = far[np.random.randint(len(far))]
    return np.exp2(a.ravel()).repeat(32)


def f64(x):
    return np.asarray(x).astype(np.float64)


def striped(idx):
    return np.tile(idx.reshape(-1, 16).T, (8, 1)).astype(np.uint16)


def unstriped(offs):
    return offs[:16].T.reshape(-1).astype(np.int64)


E2M1 = np.array([0.0, 0.5, 1.0, 1.5, 2.0, 3.0, 4.0, 6.0, -0.0, -0.5, -1.0, -1.5, -2.0, -3.0, -4.0, -6.0])


def pack_weight(w, fmt):
    k, n = w.shape
    w = f64(np.asarray(w, np.float32).astype(ml_dtypes.bfloat16)).reshape(k // 32, 32, n)
    amax = np.abs(w).max(1)
    if fmt == "e4m3":
        byte = np.frexp(amax)[1] - 1 + 127 - 7
    else:
        mant, ex = np.frexp(amax / 6.0)
        byte = np.where(mant > 0.5, ex, ex - 1) + 127
    byte = np.clip(np.where(amax > 0, byte, 1), 1, 254)
    scaled = (w * np.exp2(127.0 - byte)[:, None, :]).reshape(k, n).astype(np.float32)
    by_word = np.ascontiguousarray(scaled.reshape(k // 512, 128, 4, n).transpose(0, 1, 3, 2))
    if fmt == "e4m3":
        words = by_word.astype(ml_dtypes.float8_e4m3fn).view(np.uint8)
    else:
        c = by_word.astype(ml_dtypes.float4_e2m1fn).view(np.uint8) & 0xF
        words = (c[..., 0::2] | (c[..., 1::2] << 4)).reshape(k // 512, 128, 2 * n)
    return np.ascontiguousarray(words), np.ascontiguousarray(byte.astype(np.uint8).reshape(k // 512, 16, n))


def unpack_weight(words, scales, fmt):
    g, _, n = scales.shape
    words = np.ascontiguousarray(words).reshape(g, 128, n, -1)
    if fmt == "e4m3":
        vals = words.view(ml_dtypes.float8_e4m3fn).astype(np.float64)
    else:
        nib = np.empty((g, 128, n, 4), np.uint8)
        nib[..., 0::2] = words & 0xF
        nib[..., 1::2] = words >> 4
        vals = E2M1[nib]
    vals = vals * np.repeat(np.exp2(scales.astype(np.float64) - 127.0), 8, axis=1)[..., None]
    return vals.transpose(0, 1, 3, 2).reshape(g * 512, n)


def planes(y):
    n, m = y.shape
    v = y.astype(np.float32).astype(ml_dtypes.bfloat16).astype(np.float64).reshape(n // 32, 32, m)
    top = np.abs(v).max(1)
    byte = np.clip(np.where(top > 0, np.frexp(top)[1] - 1 + 127 - 7, 1), 1, 254)
    codes = (v * np.exp2(127.0 - byte)[:, None, :]).reshape(n, m).astype(np.float32).astype(ml_dtypes.float8_e4m3fn).view(np.uint8)
    words = codes.reshape(n // 512, 128, 4, m).transpose(0, 1, 3, 2)
    return np.ascontiguousarray(words), np.ascontiguousarray(byte.astype(np.uint8).reshape(n // 512, 16, m))


def gelu(f):
    return 0.5 * f * (1.0 + np.tanh(np.sqrt(2.0 / np.pi) * (f + 0.044715 * f**3)))


K, R, N, T, J = 512, 512, 512, 2048, 1024


def setup_inputs():
    n = np.random.standard_normal
    s = mx_kscale(K)[:, None]
    u = mx_kscale(R)[:, None]
    p_tab = pack_weight(n((K, T)) * s, "e4m3")
    p_wg = pack_weight(n((K, R)) / np.sqrt(K) / s, "e2m1")
    return {
        "tab_words": p_tab[0],
        "tab_scales": p_tab[1],
        "wg_words": p_wg[0],
        "wg_scales": p_wg[1],
        "wu": (n((K, R)) / np.sqrt(K) / s * u.T).astype(np.float32),
        "wd": (n((R, N)) / np.sqrt(R) / u).astype(np.float32),
        "gT": (n((N, T))).astype(np.float32),
        "wgo": np.tile(np.random.uniform(0.5, 2.0, J), (128, 1)).astype(np.float32),
        "offs": striped(np.random.permutation(T)[:J]),
    }


def reference(tab_words, tab_scales, wg_words, wg_scales, wu, wd, gT, wgo, offs):
    idx = unstriped(offs)
    tab_ = unpack_weight(tab_words, tab_scales, "e4m3")[:, idx]
    wg_ = unpack_weight(wg_words, wg_scales, "e2m1")
    wu_ = mxq(f64(wu), 0, "e4m3")
    ga = wg_.T @ tab_
    ub = wu_.T @ tab_
    h = gelu(ga) * ub
    h_ = mxq(h, 0, "e4m3")
    wd_ = mxq(f64(wd), 0, "e4m3")
    y = wd_.T @ h_
    out = np.zeros((N, T))
    out[:, idx] = f64(wgo)[0] * (y * f64(gT)[:, idx])
    return (out,) + planes(out)

@@ -1,0 +1,214 @@
+from contextlib import ExitStack
+
+import concourse.mybir as mybir
+
+K, R, N, T, J = 512, 512, 512, 2048, 1024
+FLOPS = 2 * J * (2 * K * R + R * N)
+
+F32 = mybir.dt.float32
+BF16 = mybir.dt.bfloat16
+I32 = mybir.dt.int32
+U32 = mybir.dt.uint32
+U16 = mybir.dt.uint16
+U8 = mybir.dt.uint8
+FP8X4 = mybir.dt.float8_e4m3fn_x4
+FP4X4 = mybir.dt.float4_e2m1fn_x4
+MULT = mybir.AluOpType.mult
+GELU = mybir.ActivationFunctionType.Gelu_apprx_tanh
+
+P = 128
+PACK = 4
+HALF = 512
+CHUNK = 128
+OUT_COLS = 512
+VECTOR_TILES = 2
+
+
+def tile_list_modp_ggelu_gateP_kernel(
+    tc, tab_words, tab_scales, wg_words, wg_scales, wu, wd, gT, wgo, offs, out_0, out_1, out_2
+):
+    nc = tc.nc
+    halves = J // HALF
+    chunks = HALF // CHUNK
+    with ExitStack() as ctx:
+        keep = ctx.enter_context(tc.tile_pool(name="keep", bufs=1))
+        ring = ctx.enter_context(tc.tile_pool(name="ring", bufs=2))
+        deep = ctx.enter_context(tc.tile_pool(name="deep", bufs=4))
+        psum = ctx.enter_context(tc.psum_pool(name="psum", bufs=3))
+        psum_y = ctx.enter_context(tc.psum_pool(name="psum_y", bufs=2))
+
+        offsets = keep.tile([P, J // 16], U16, name="offsets")
+        nc.sync.dma_start(offsets[:], offs)
+
+        def listed(h):
+            return offsets[:, h * HALF // 16 : (h + 1) * HALF // 16]
+
+        tab_plane = keep.tile([P, T], U8, name="tab_plane", tag="gate3", align_bytes=64)
+        wg_plane = keep.tile([P, R], U8, name="wg_plane", tag="wgo", align_bytes=64)
+        nc.gpsimd.memset(tab_plane[:].bitcast(I32), 0)
+        warm = keep.tile([P, 1], F32, name="warm")
+        warm_out = keep.tile([P, 1], F32, name="warm_out")
+        nc.vector.memset(warm[:], 0.0)
+        nc.gpsimd.memset(wg_plane[:].bitcast(I32), 0)
+        for q in range(4):
+            nc.scalar.dma_start(tab_plane[32 * q : 32 * q + 4, :].bitcast(I32), tab_scales[0, 4 * q : 4 * q + 4, :].bitcast(I32))
+        nc.scalar.activation(warm_out[:], warm[:], GELU)
+        for q in range(4):
+            nc.gpsimd.dma_start(wg_plane[32 * q : 32 * q + 4, :].bitcast(I32), wg_scales[0, 4 * q : 4 * q + 4, :].bitcast(I32))
+
+        wu_raw = keep.tile([P, PACK, R], F32, name="wu_raw", tag="gate0", align_bytes=64)
+        nc.sync.dma_start(wu_raw[:], wu.rearrange("(p j) c -> p j c", j=PACK))
+        tab_codes = keep.tile([P, T], I32, name="tab_codes", tag="gate1", align_bytes=64)
+        nc.sync.dma_start(tab_codes[:], tab_words[0].rearrange("p t i -> p (t i)").bitcast(I32))
+        wg_raw = keep.tile([P, R // 2], I32, name="wg_raw", tag="gate2", align_bytes=64)
+        nc.sync.dma_start(wg_raw[:], wg_words[0].bitcast(I32))
+
+        pages = []
+        page = keep.tile([P, T], F32, name="page", tag="page0")
+        nc.vector.memset(page[:].bitcast(I32), 0)
+        pages.append(page)
+
+        wu_bf = keep.tile([P, PACK * R], BF16, name="wu_bf", align_bytes=64)
+        nc.scalar.copy(
+            wu_bf[:].rearrange("p (t m i j) -> p m t j i", t=PACK, i=4, j=PACK),
+            wu_raw[:].rearrange("p j (m t i) -> p m t j i", t=PACK, i=4),
+        )
+        wu_codes = keep.tile([P, R], U32, name="wu_codes", align_bytes=64)
+        wu_sc = keep.tile([P, R], U8, name="wu_sc", align_bytes=64)
+
+        v_codes, v_sc = [], []
+        for h in range(halves):
+            sc = keep.tile([P, HALF], U8, name=f"v_sc{h}", align_bytes=64)
+            nc.vector.tensor_copy(sc[:], tab_plane[:].indirect(listed(h)))
+            v_sc.append(sc)
+
+        wg_codes = keep.tile([P, 2 * R], U8, name="wg_codes", align_bytes=64)
+        wg_sc = keep.tile([P, R], U8, name="wg_sc", align_bytes=64)
+        nc.vector.tensor_copy(
+            wg_codes[:].bitcast(I32).rearrange("p (t m u) -> p t m u", t=PACK, u=2),
+            wg_raw[:].rearrange("p (m t u) -> p t m u", t=PACK, u=2),
+        )
+        nc.vector.tensor_copy(
+            wg_sc[:].bitcast(I32).rearrange("p (t m) -> p t m", t=PACK),
+            wg_plane[:].bitcast(I32).rearrange("p (m t) -> p t m", t=PACK),
+        )
+
+        wd_raw = keep.tile([P, PACK, N], F32, name="wd_raw", tag="gate2", align_bytes=64)
+        wd_rows = wd.rearrange("(m s i) n -> i m s n", s=PACK, i=4)
+        for i in range(4):
+            nc.sync.dma_start(wd_raw[i:P:4, :, :], wd_rows[i])
+        wgo_sb = keep.tile([P, J], F32, name="wgo_sb", tag="wgo", align_bytes=64)
+        nc.sync.dma_start(wgo_sb[:], wgo)
+
+        for h in range(halves):
+            codes = keep.tile([P, HALF], U32, name=f"v_codes{h}", align_bytes=64)
+            nc.vector.tensor_copy(codes[:], tab_codes[:].bitcast(U32).indirect(listed(h)))
+            v_codes.append(codes)
+            if h == 0:
+                nc.vector.quantize_mx(wu_codes[:].bitcast(FP8X4), wu_sc[:], wu_bf[:])
+
+        wd_bf = keep.tile([P, PACK * N], BF16, name="wd_bf", align_bytes=64)
+        wd_codes = keep.tile([P, N], U32, name="wd_codes", align_bytes=64)
+        wd_sc = keep.tile([P, N], U8, name="wd_sc", align_bytes=64)
+
+        h_codes, h_sc = [], []
+        for h in range(halves):
+            h_bf = keep.tile([P, PACK * HALF], BF16, name=f"h_bf{h}", align_bytes=64)
+            for c in range(chunks):
+                cols = slice(c * CHUNK, (c + 1) * CHUNK)
+                ga = psum.tile([P, PACK, CHUNK], F32, name="ga")
+                for t in range(PACK):
+                    nc.tensor.matmul_mx(
+                        ga[:, t, :],
+                        lhsT=wg_codes[:, 2 * P * t : 2 * P * (t + 1)].bitcast(FP4X4),
+                        lhsT_scale=wg_sc[:, P * t : P * (t + 1)],
+                        rhs=v_codes[h][:, cols].bitcast(FP8X4),
+                        rhs_scale=v_sc[h][:, cols],
+                        start=True,
+                        stop=True,
+                    )
+                ub = psum.tile([P, PACK, CHUNK], F32, name="ub")
+                for t in range(PACK):
+                    nc.tensor.matmul_mx(
+                        ub[:, t, :],
+                        lhsT=wu_codes[:, P * t : P * (t + 1)].bitcast(FP8X4),
+                        lhsT_scale=wu_sc[:, P * t : P * (t + 1)],
+                        rhs=v_codes[h][:, cols].bitcast(FP8X4),
+                        rhs_scale=v_sc[h][:, cols],
+                        start=True,
+                        stop=True,
+                    )
+                act = deep.tile([P, CHUNK, PACK], F32, name="act")
+                nc.scalar.activation(act[:], ga[:].rearrange("p t j -> p j t"), GELU)
+                nc.vector.tensor_tensor(
+                    h_bf[:, PACK * c * CHUNK : PACK * (c + 1) * CHUNK].rearrange("p (j t) -> p j t", t=PACK),
+                    ub[:].rearrange("p t j -> p j t"),
+                    act[:],
+                    MULT,
+                )
+            codes = keep.tile([P, HALF], U32, name=f"h_codes{h}", align_bytes=64)
+            sc = keep.tile([P, HALF], U8, name=f"h_sc{h}", align_bytes=64)
+            nc.vector.quantize_mx(codes[:].bitcast(FP8X4), sc[:], h_bf[:])
+            h_codes.append(codes)
+            h_sc.append(sc)
+
+        nc.scalar.copy(
+            wd_bf[:].rearrange("p (t m s) -> p m s t", t=PACK, s=PACK),
+            wd_raw[:].rearrange("p s (m t) -> p m s t", t=PACK),
+        )
+        nc.vector.quantize_mx(wd_codes[:].bitcast(FP8X4), wd_sc[:], wd_bf[:])
+
+        gates = []
+        gT_rows = gT.rearrange("(p t) c -> t p c", t=PACK)
+        for t in range(PACK):
+            gate = keep.tile([P, T], F32, name="gate", tag=f"gate{t}", align_bytes=64)
+            nc.sync.dma_start(gate[:], gT_rows[t])
+            gates.append(gate)
+
+        out_tiles = T // OUT_COLS
+        out_bf = [keep.tile([P, OUT_COLS, PACK], BF16, name=f"out_bf{a}", align_bytes=64) for a in range(out_tiles)]
+        out_rows = out_0.rearrange("(p t) c -> t p c", t=PACK)
+        for t in range(PACK):
+            for h in range(halves):
+                y_ps = psum_y.tile([P, HALF], F32, name="y_ps")
+                nc.tensor.matmul_mx(
+                    y_ps[:],
+                    lhsT=wd_codes[:, P * t : P * (t + 1)].bitcast(FP8X4),
+                    lhsT_scale=wd_sc[:, P * t : P * (t + 1)],
+                    rhs=h_codes[h][:].bitcast(FP8X4),
+                    rhs_scale=h_sc[h][:],
+                    start=True,
+                    stop=True,
+                )
+                step = t * halves + h
+                if step + 1 < PACK:
+                    y = keep.tile([P, HALF], F32, name="y_first", tag=f"page{step + 1}")
+                else:
+                    y = deep.tile([P, HALF], F32, name="y")
+                nc.scalar.copy(y[:], y_ps[:])
+                gw = ring.tile([P, HALF], F32, name="gw")
+                nc.vector.tensor_tensor(gw[:], gates[t][:].indirect(listed(h)), wgo_sb[:, h * HALF : (h + 1) * HALF], MULT)
+                nc.vector.tensor_tensor(pages[t][:].indirect(listed(h)), y[:], gw[:], MULT)
+                if step + 1 < PACK:
+                    page = keep.tile([P, T], F32, name="page", tag=f"page{step + 1}")
+                    nc.gpsimd.memset(page[:], 0.0)
+                    pages.append(page)
+            nc.sync.dma_start(out_rows[t], pages[t][:])
+            for a in range(out_tiles):
+                src = pages[t][:, a * OUT_COLS : (a + 1) * OUT_COLS]
+                if a < VECTOR_TILES and t == PACK - 1:
+                    nc.vector.tensor_copy(out_bf[a][:, :, t], src)
+                elif a < VECTOR_TILES and t == PACK - 2:
+                    nc.scalar.copy(out_bf[a][:, :, t : t + 2], src.unsqueeze(2).to_broadcast([P, OUT_COLS, 2]))
+                else:
+                    nc.scalar.copy(out_bf[a][:, :, t], src)
+
+        out_sc = keep.tile([P, T], U8, name="out_sc", align_bytes=64)
+        out_words = out_1[0].rearrange("p t i -> p (t i)").bitcast(I32)
+        for a in range(out_tiles):
+            cols = slice(a * OUT_COLS, (a + 1) * OUT_COLS)
+            out_codes = keep.tile([P, OUT_COLS], I32, name=f"out_codes{a}", align_bytes=64)
+            nc.vector.quantize_mx(out_codes[:].bitcast(FP8X4), out_sc[:, cols], out_bf[a][:].rearrange("p c t -> p (c t)"))
+            nc.sync.dma_start(out_words[:, cols], out_codes[:])
+        for q in range(4):
+            nc.scalar.dma_start(out_2[0, 4 * q : 4 * q + 4, :].bitcast(I32), out_sc[32 * q : 32 * q + 4, :].bitcast(I32))

@@ -22,6 +22,7 @@ HALF = 512
 CHUNK = 128
 OUT_COLS = 512
 VECTOR_TILES = 2
+EARLY_PAGES = 1
 
 
 def tile_list_modp_ggelu_gateP_kernel(
@@ -32,8 +33,7 @@ def tile_list_modp_ggelu_gateP_kernel(
     chunks = HALF // CHUNK
     with ExitStack() as ctx:
         keep = ctx.enter_context(tc.tile_pool(name="keep", bufs=1))
-        ring = ctx.enter_context(tc.tile_pool(name="ring", bufs=2))
-        deep = ctx.enter_context(tc.tile_pool(name="deep", bufs=4))
+        ring = ctx.enter_context(tc.tile_pool(name="ring", bufs=3))
         psum = ctx.enter_context(tc.psum_pool(name="psum", bufs=3))
         psum_y = ctx.enter_context(tc.psum_pool(name="psum_y", bufs=2))
 
@@ -43,44 +43,34 @@ def tile_list_modp_ggelu_gateP_kernel(
         def listed(h):
             return offsets[:, h * HALF // 16 : (h + 1) * HALF // 16]
 
-        tab_plane = keep.tile([P, T], U8, name="tab_plane", tag="gate3", align_bytes=64)
+        tab_plane = keep.tile([P, T], U8, name="tab_plane", tag="gate0", align_bytes=64)
         wg_plane = keep.tile([P, R], U8, name="wg_plane", tag="wgo", align_bytes=64)
         nc.gpsimd.memset(tab_plane[:].bitcast(I32), 0)
+        nc.gpsimd.memset(wg_plane[:].bitcast(I32), 0)
         warm = keep.tile([P, 1], F32, name="warm")
         warm_out = keep.tile([P, 1], F32, name="warm_out")
         nc.vector.memset(warm[:], 0.0)
-        nc.gpsimd.memset(wg_plane[:].bitcast(I32), 0)
-        for q in range(4):
-            nc.scalar.dma_start(tab_plane[32 * q : 32 * q + 4, :].bitcast(I32), tab_scales[0, 4 * q : 4 * q + 4, :].bitcast(I32))
         nc.scalar.activation(warm_out[:], warm[:], GELU)
-        for q in range(4):
-            nc.gpsimd.dma_start(wg_plane[32 * q : 32 * q + 4, :].bitcast(I32), wg_scales[0, 4 * q : 4 * q + 4, :].bitcast(I32))
 
-        wu_raw = keep.tile([P, PACK, R], F32, name="wu_raw", tag="gate0", align_bytes=64)
-        nc.sync.dma_start(wu_raw[:], wu.rearrange("(p j) c -> p j c", j=PACK))
+        wg_raw = keep.tile([P, R // 2], I32, name="wg_raw", tag="gate3", align_bytes=64)
+        nc.sync.dma_start(wg_raw[:], wg_words[0].bitcast(I32))
+        for q in range(4):
+            nc.sync.dma_start(tab_plane[32 * q : 32 * q + 4, :].bitcast(I32), tab_scales[0, 4 * q : 4 * q + 4, :].bitcast(I32))
         tab_codes = keep.tile([P, T], I32, name="tab_codes", tag="gate1", align_bytes=64)
         nc.sync.dma_start(tab_codes[:], tab_words[0].rearrange("p t i -> p (t i)").bitcast(I32))
-        wg_raw = keep.tile([P, R // 2], I32, name="wg_raw", tag="gate2", align_bytes=64)
-        nc.sync.dma_start(wg_raw[:], wg_words[0].bitcast(I32))
+        wu_rows = wu.rearrange("(p j) c -> p j c", j=PACK)
+        wu_lo = keep.tile([P, PACK, R // 2], F32, name="wu_lo")
+        nc.sync.dma_start(wu_lo[:], wu_rows[:, :, : R // 2])
+        for q in range(4):
+            nc.sync.dma_start(wg_plane[32 * q : 32 * q + 4, :].bitcast(I32), wg_scales[0, 4 * q : 4 * q + 4, :].bitcast(I32))
+        wu_hi = keep.tile([P, PACK, R // 2], F32, name="wu_hi", tag="gate2", align_bytes=64)
+        nc.sync.dma_start(wu_hi[:], wu_rows[:, :, R // 2 :])
 
         pages = []
-        page = keep.tile([P, T], F32, name="page", tag="page0")
-        nc.vector.memset(page[:].bitcast(I32), 0)
-        pages.append(page)
-
-        wu_bf = keep.tile([P, PACK * R], BF16, name="wu_bf", align_bytes=64)
-        nc.scalar.copy(
-            wu_bf[:].rearrange("p (t m i j) -> p m t j i", t=PACK, i=4, j=PACK),
-            wu_raw[:].rearrange("p j (m t i) -> p m t j i", t=PACK, i=4),
-        )
-        wu_codes = keep.tile([P, R], U32, name="wu_codes", align_bytes=64)
-        wu_sc = keep.tile([P, R], U8, name="wu_sc", align_bytes=64)
-
-        v_codes, v_sc = [], []
-        for h in range(halves):
-            sc = keep.tile([P, HALF], U8, name=f"v_sc{h}", align_bytes=64)
-            nc.vector.tensor_copy(sc[:], tab_plane[:].indirect(listed(h)))
-            v_sc.append(sc)
+        for t in range(EARLY_PAGES):
+            page = keep.tile([P, T], F32, name="page", tag=f"page{t}")
+            nc.vector.memset(page[:].bitcast(I32), 0)
+            pages.append(page)
 
         wg_codes = keep.tile([P, 2 * R], U8, name="wg_codes", align_bytes=64)
         wg_sc = keep.tile([P, R], U8, name="wg_sc", align_bytes=64)
@@ -88,26 +78,34 @@ def tile_list_modp_ggelu_gateP_kernel(
             wg_codes[:].bitcast(I32).rearrange("p (t m u) -> p t m u", t=PACK, u=2),
             wg_raw[:].rearrange("p (m t u) -> p t m u", t=PACK, u=2),
         )
-        nc.vector.tensor_copy(
-            wg_sc[:].bitcast(I32).rearrange("p (t m) -> p t m", t=PACK),
-            wg_plane[:].bitcast(I32).rearrange("p (m t) -> p t m", t=PACK),
-        )
-
-        wd_raw = keep.tile([P, PACK, N], F32, name="wd_raw", tag="gate2", align_bytes=64)
+        wd_raw = keep.tile([P, PACK, N], F32, name="wd_raw", tag="gate3", align_bytes=64)
         wd_rows = wd.rearrange("(m s i) n -> i m s n", s=PACK, i=4)
         for i in range(4):
             nc.sync.dma_start(wd_raw[i:P:4, :, :], wd_rows[i])
-        wgo_sb = keep.tile([P, J], F32, name="wgo_sb", tag="wgo", align_bytes=64)
-        nc.sync.dma_start(wgo_sb[:], wgo)
 
+        v_sc = keep.tile([P, J], U8, name="v_sc", align_bytes=64)
+        nc.vector.tensor_copy(v_sc[:], tab_plane[:].indirect(offsets[:]))
+        v_codes = []
         for h in range(halves):
             codes = keep.tile([P, HALF], U32, name=f"v_codes{h}", align_bytes=64)
             nc.vector.tensor_copy(codes[:], tab_codes[:].bitcast(U32).indirect(listed(h)))
             v_codes.append(codes)
             if h == 0:
-                nc.vector.quantize_mx(wu_codes[:].bitcast(FP8X4), wu_sc[:], wu_bf[:])
+                nc.vector.tensor_copy(
+                    wg_sc[:].bitcast(I32).rearrange("p (t m) -> p t m", t=PACK),
+                    wg_plane[:].bitcast(I32).rearrange("p (m t) -> p t m", t=PACK),
+                )
+        wgo_sb = keep.tile([P, J], F32, name="wgo_sb", tag="wgo", align_bytes=64)
+        nc.sync.dma_start(wgo_sb[:], wgo)
 
-        wd_bf = keep.tile([P, PACK * N], BF16, name="wd_bf", align_bytes=64)
+        wu_bf = keep.tile([P, PACK * R], BF16, name="wu_bf", align_bytes=64)
+        wu_dealt = wu_bf[:].rearrange("p (t m i j) -> p m t j i", t=PACK, i=4, j=PACK)
+        nc.scalar.copy(wu_dealt[:, :16], wu_lo[:].rearrange("p j (m t i) -> p m t j i", t=PACK, i=4))
+        nc.vector.tensor_copy(wu_dealt[:, 16:], wu_hi[:].rearrange("p j (m t i) -> p m t j i", t=PACK, i=4))
+        wu_codes = keep.tile([P, R], U32, name="wu_codes", align_bytes=64)
+        wu_sc = keep.tile([P, R], U8, name="wu_sc", align_bytes=64)
+        nc.vector.quantize_mx(wu_codes[:].bitcast(FP8X4), wu_sc[:], wu_bf[:])
+
         wd_codes = keep.tile([P, N], U32, name="wd_codes", align_bytes=64)
         wd_sc = keep.tile([P, N], U8, name="wd_sc", align_bytes=64)
 
@@ -123,7 +121,7 @@ def tile_list_modp_ggelu_gateP_kernel(
                         lhsT=wg_codes[:, 2 * P * t : 2 * P * (t + 1)].bitcast(FP4X4),
                         lhsT_scale=wg_sc[:, P * t : P * (t + 1)],
                         rhs=v_codes[h][:, cols].bitcast(FP8X4),
-                        rhs_scale=v_sc[h][:, cols],
+                        rhs_scale=v_sc[:, h * HALF + c * CHUNK : h * HALF + (c + 1) * CHUNK],
                         start=True,
                         stop=True,
                     )
@@ -134,11 +132,11 @@ def tile_list_modp_ggelu_gateP_kernel(
                         lhsT=wu_codes[:, P * t : P * (t + 1)].bitcast(FP8X4),
                         lhsT_scale=wu_sc[:, P * t : P * (t + 1)],
                         rhs=v_codes[h][:, cols].bitcast(FP8X4),
-                        rhs_scale=v_sc[h][:, cols],
+                        rhs_scale=v_sc[:, h * HALF + c * CHUNK : h * HALF + (c + 1) * CHUNK],
                         start=True,
                         stop=True,
                     )
-                act = deep.tile([P, CHUNK, PACK], F32, name="act")
+                act = keep.tile([P, CHUNK, PACK], F32, name="act", tag=f"act{h * chunks + c}", align_bytes=64)
                 nc.scalar.activation(act[:], ga[:].rearrange("p t j -> p j t"), GELU)
                 nc.vector.tensor_tensor(
                     h_bf[:, PACK * c * CHUNK : PACK * (c + 1) * CHUNK].rearrange("p (j t) -> p j t", t=PACK),
@@ -152,6 +150,7 @@ def tile_list_modp_ggelu_gateP_kernel(
             h_codes.append(codes)
             h_sc.append(sc)
 
+        wd_bf = keep.tile([P, PACK * N], BF16, name="wd_bf", tag=f"act{chunks}", align_bytes=64)
         nc.scalar.copy(
             wd_bf[:].rearrange("p (t m s) -> p m s t", t=PACK, s=PACK),
             wd_raw[:].rearrange("p s (m t) -> p m s t", t=PACK),
@@ -181,16 +180,14 @@ def tile_list_modp_ggelu_gateP_kernel(
                     stop=True,
                 )
                 step = t * halves + h
-                if step + 1 < PACK:
-                    y = keep.tile([P, HALF], F32, name="y_first", tag=f"page{step + 1}")
-                else:
-                    y = deep.tile([P, HALF], F32, name="y")
+                late = EARLY_PAGES + step
+                y = keep.tile([P, HALF], F32, name="y", tag=f"page{late}" if late < PACK else f"y{step}")
                 nc.scalar.copy(y[:], y_ps[:])
                 gw = ring.tile([P, HALF], F32, name="gw")
                 nc.vector.tensor_tensor(gw[:], gates[t][:].indirect(listed(h)), wgo_sb[:, h * HALF : (h + 1) * HALF], MULT)
                 nc.vector.tensor_tensor(pages[t][:].indirect(listed(h)), y[:], gw[:], MULT)
-                if step + 1 < PACK:
-                    page = keep.tile([P, T], F32, name="page", tag=f"page{step + 1}")
+                if late < PACK:
+                    page = keep.tile([P, T], F32, name="page", tag=f"page{late}")
                     nc.gpsimd.memset(page[:], 0.0)
                     pages.append(page)
             nc.sync.dma_start(out_rows[t], pages[t][:])

@@ -20,9 +20,8 @@ P = 128
 PACK = 4
 HALF = 512
 CHUNK = 128
-OUT_COLS = 512
-VECTOR_TILES = 2
 EARLY_PAGES = 1
+LEAD = 3
 
 
 def tile_list_modp_ggelu_gateP_kernel(
@@ -33,8 +32,8 @@ def tile_list_modp_ggelu_gateP_kernel(
     chunks = HALF // CHUNK
     with ExitStack() as ctx:
         keep = ctx.enter_context(tc.tile_pool(name="keep", bufs=1))
-        ring = ctx.enter_context(tc.tile_pool(name="ring", bufs=3))
-        psum = ctx.enter_context(tc.psum_pool(name="psum", bufs=3))
+        ring = ctx.enter_context(tc.tile_pool(name="ring", bufs=2))
+        psum = ctx.enter_context(tc.psum_pool(name="psum", bufs=1))
         psum_y = ctx.enter_context(tc.psum_pool(name="psum_y", bufs=2))
 
         offsets = keep.tile([P, J // 16], U16, name="offsets")
@@ -44,7 +43,7 @@ def tile_list_modp_ggelu_gateP_kernel(
             return offsets[:, h * HALF // 16 : (h + 1) * HALF // 16]
 
         tab_plane = keep.tile([P, T], U8, name="tab_plane", tag="gate0", align_bytes=64)
-        wg_plane = keep.tile([P, R], U8, name="wg_plane", tag="wgo", align_bytes=64)
+        wg_plane = keep.tile([P, R], U8, name="wg_plane", tag="wd_raw", align_bytes=64)
         nc.gpsimd.memset(tab_plane[:].bitcast(I32), 0)
         nc.gpsimd.memset(wg_plane[:].bitcast(I32), 0)
         warm = keep.tile([P, 1], F32, name="warm")
@@ -52,14 +51,14 @@ def tile_list_modp_ggelu_gateP_kernel(
         nc.vector.memset(warm[:], 0.0)
         nc.scalar.activation(warm_out[:], warm[:], GELU)
 
-        wg_raw = keep.tile([P, R // 2], I32, name="wg_raw", tag="gate3", align_bytes=64)
+        wg_raw = keep.tile([P, R // 2], I32, name="wg_raw", tag="wgo", align_bytes=64)
         nc.sync.dma_start(wg_raw[:], wg_words[0].bitcast(I32))
         for q in range(4):
             nc.sync.dma_start(tab_plane[32 * q : 32 * q + 4, :].bitcast(I32), tab_scales[0, 4 * q : 4 * q + 4, :].bitcast(I32))
         tab_codes = keep.tile([P, T], I32, name="tab_codes", tag="gate1", align_bytes=64)
         nc.sync.dma_start(tab_codes[:], tab_words[0].rearrange("p t i -> p (t i)").bitcast(I32))
         wu_rows = wu.rearrange("(p j) c -> p j c", j=PACK)
-        wu_lo = keep.tile([P, PACK, R // 2], F32, name="wu_lo")
+        wu_lo = keep.tile([P, PACK, R // 2], F32, name="wu_lo", tag="gate3", align_bytes=64)
         nc.sync.dma_start(wu_lo[:], wu_rows[:, :, : R // 2])
         for q in range(4):
             nc.sync.dma_start(wg_plane[32 * q : 32 * q + 4, :].bitcast(I32), wg_scales[0, 4 * q : 4 * q + 4, :].bitcast(I32))
@@ -78,10 +77,8 @@ def tile_list_modp_ggelu_gateP_kernel(
             wg_codes[:].bitcast(I32).rearrange("p (t m u) -> p t m u", t=PACK, u=2),
             wg_raw[:].rearrange("p (m t u) -> p t m u", t=PACK, u=2),
         )
-        wd_raw = keep.tile([P, PACK, N], F32, name="wd_raw", tag="gate3", align_bytes=64)
-        wd_rows = wd.rearrange("(m s i) n -> i m s n", s=PACK, i=4)
-        for i in range(4):
-            nc.sync.dma_start(wd_raw[i:P:4, :, :], wd_rows[i])
+        wgo_sb = keep.tile([P, J], F32, name="wgo_sb", tag="wgo", align_bytes=64)
+        nc.sync.dma_start(wgo_sb[:], wgo)
 
         v_sc = keep.tile([P, J], U8, name="v_sc", align_bytes=64)
         nc.vector.tensor_copy(v_sc[:], tab_plane[:].indirect(offsets[:]))
@@ -95,8 +92,10 @@ def tile_list_modp_ggelu_gateP_kernel(
                     wg_sc[:].bitcast(I32).rearrange("p (t m) -> p t m", t=PACK),
                     wg_plane[:].bitcast(I32).rearrange("p (m t) -> p t m", t=PACK),
                 )
-        wgo_sb = keep.tile([P, J], F32, name="wgo_sb", tag="wgo", align_bytes=64)
-        nc.sync.dma_start(wgo_sb[:], wgo)
+        wd_raw = keep.tile([P, PACK, N], F32, name="wd_raw", tag="wd_raw", align_bytes=64)
+        wd_rows = wd.rearrange("(m s i) n -> i m s n", s=PACK, i=4)
+        for i in range(4):
+            nc.sync.dma_start(wd_raw[i:P:4, :, :], wd_rows[i])
 
         wu_bf = keep.tile([P, PACK * R], BF16, name="wu_bf", align_bytes=64)
         wu_dealt = wu_bf[:].rearrange("p (t m i j) -> p m t j i", t=PACK, i=4, j=PACK)
@@ -106,15 +105,34 @@ def tile_list_modp_ggelu_gateP_kernel(
         wu_sc = keep.tile([P, R], U8, name="wu_sc", align_bytes=64)
         nc.vector.quantize_mx(wu_codes[:].bitcast(FP8X4), wu_sc[:], wu_bf[:])
 
-        wd_codes = keep.tile([P, N], U32, name="wd_codes", align_bytes=64)
         wd_sc = keep.tile([P, N], U8, name="wd_sc", align_bytes=64)
 
+        gT_rows = gT.rearrange("(p t) c -> t p c", t=PACK)
+        gates = []
+        for t in range(PACK):
+            gate = keep.tile([P, T], F32, name="gate", tag=f"gate{t}", align_bytes=64)
+            nc.sync.dma_start(gate[:], gT_rows[t])
+            gates.append(gate)
+
+        def weighted_gate(t):
+            gw = ring.tile([P, J], F32, name="gw")
+            nc.vector.tensor_tensor(gw[:], gates[t][:].indirect(offsets[:]), wgo_sb[:], MULT)
+            return gw
+
+        def late_page(tag):
+            page = keep.tile([P, T], F32, name="page", tag=tag, align_bytes=64)
+            nc.gpsimd.memset(page[:], 0.0)
+            pages.append(page)
+
+        gws = []
         h_codes, h_sc = [], []
         for h in range(halves):
             h_bf = keep.tile([P, PACK * HALF], BF16, name=f"h_bf{h}", align_bytes=64)
             for c in range(chunks):
                 cols = slice(c * CHUNK, (c + 1) * CHUNK)
-                ga = psum.tile([P, PACK, CHUNK], F32, name="ga")
+                n = h * chunks + c
+                turn = (n // LEAD) % 2
+                ga = psum.tile([P, PACK, CHUNK], F32, name="ga", tag=f"bank{turn}_{n % LEAD}")
                 for t in range(PACK):
                     nc.tensor.matmul_mx(
                         ga[:, t, :],
@@ -125,7 +143,7 @@ def tile_list_modp_ggelu_gateP_kernel(
                         start=True,
                         stop=True,
                     )
-                ub = psum.tile([P, PACK, CHUNK], F32, name="ub")
+                ub = psum.tile([P, PACK, CHUNK], F32, name="ub", tag=f"bank{1 - turn}_{n % LEAD}")
                 for t in range(PACK):
                     nc.tensor.matmul_mx(
                         ub[:, t, :],
@@ -136,7 +154,7 @@ def tile_list_modp_ggelu_gateP_kernel(
                         start=True,
                         stop=True,
                     )
-                act = keep.tile([P, CHUNK, PACK], F32, name="act", tag=f"act{h * chunks + c}", align_bytes=64)
+                act = keep.tile([P, CHUNK, PACK], F32, name="act", tag=f"act{n}", align_bytes=64)
                 nc.scalar.activation(act[:], ga[:].rearrange("p t j -> p j t"), GELU)
                 nc.vector.tensor_tensor(
                     h_bf[:, PACK * c * CHUNK : PACK * (c + 1) * CHUNK].rearrange("p (j t) -> p j t", t=PACK),
@@ -155,19 +173,14 @@ def tile_list_modp_ggelu_gateP_kernel(
             wd_bf[:].rearrange("p (t m s) -> p m s t", t=PACK, s=PACK),
             wd_raw[:].rearrange("p s (m t) -> p m s t", t=PACK),
         )
+
+        gws.append(weighted_gate(0))
+        wd_codes = keep.tile([P, N], U32, name="wd_codes", tag="gate0", align_bytes=64)
         nc.vector.quantize_mx(wd_codes[:].bitcast(FP8X4), wd_sc[:], wd_bf[:])
-
-        gates = []
-        gT_rows = gT.rearrange("(p t) c -> t p c", t=PACK)
+        late_page(f"act{chunks}")
+        ys = []
         for t in range(PACK):
-            gate = keep.tile([P, T], F32, name="gate", tag=f"gate{t}", align_bytes=64)
-            nc.sync.dma_start(gate[:], gT_rows[t])
-            gates.append(gate)
-
-        out_tiles = T // OUT_COLS
-        out_bf = [keep.tile([P, OUT_COLS, PACK], BF16, name=f"out_bf{a}", align_bytes=64) for a in range(out_tiles)]
-        out_rows = out_0.rearrange("(p t) c -> t p c", t=PACK)
-        for t in range(PACK):
+            y = keep.tile([P, J], F32, name=f"y{t}")
             for h in range(halves):
                 y_ps = psum_y.tile([P, HALF], F32, name="y_ps")
                 nc.tensor.matmul_mx(
@@ -179,33 +192,34 @@ def tile_list_modp_ggelu_gateP_kernel(
                     start=True,
                     stop=True,
                 )
-                step = t * halves + h
-                late = EARLY_PAGES + step
-                y = keep.tile([P, HALF], F32, name="y", tag=f"page{late}" if late < PACK else f"y{step}")
-                nc.scalar.copy(y[:], y_ps[:])
-                gw = ring.tile([P, HALF], F32, name="gw")
-                nc.vector.tensor_tensor(gw[:], gates[t][:].indirect(listed(h)), wgo_sb[:, h * HALF : (h + 1) * HALF], MULT)
-                nc.vector.tensor_tensor(pages[t][:].indirect(listed(h)), y[:], gw[:], MULT)
-                if late < PACK:
-                    page = keep.tile([P, T], F32, name="page", tag=f"page{late}")
-                    nc.gpsimd.memset(page[:], 0.0)
-                    pages.append(page)
+                nc.scalar.copy(y[:, h * HALF : (h + 1) * HALF], y_ps[:])
+            ys.append(y)
+
+        spans = [slice(0, T // 2), slice(T // 2, 3 * T // 4), slice(3 * T // 4, T)]
+        out_bf = [keep.tile([P, s.stop - s.start, PACK], BF16, name=f"out_bf{a}", align_bytes=64) for a, s in enumerate(spans)]
+        out_rows = out_0.rearrange("(p t) c -> t p c", t=PACK)
+        for t in range(PACK):
+            if t + 1 < PACK:
+                gws.append(weighted_gate(t + 1))
+            if t + 2 < PACK:
+                late_page(f"gate{t + 1}")
+            nc.vector.tensor_tensor(pages[t][:].indirect(offsets[:]), ys[t][:], gws[t][:], MULT)
             nc.sync.dma_start(out_rows[t], pages[t][:])
-            for a in range(out_tiles):
-                src = pages[t][:, a * OUT_COLS : (a + 1) * OUT_COLS]
-                if a < VECTOR_TILES and t == PACK - 1:
+            for a, s in enumerate(spans):
+                src = pages[t][:, s]
+                if a == 0 and t == PACK - 1:
                     nc.vector.tensor_copy(out_bf[a][:, :, t], src)
-                elif a < VECTOR_TILES and t == PACK - 2:
-                    nc.scalar.copy(out_bf[a][:, :, t : t + 2], src.unsqueeze(2).to_broadcast([P, OUT_COLS, 2]))
+                elif a == 0 and t == PACK - 2:
+                    nc.scalar.copy(out_bf[a][:, :, t : t + 2], src.unsqueeze(2).to_broadcast([P, T // 2, 2]))
                 else:
                     nc.scalar.copy(out_bf[a][:, :, t], src)
 
         out_sc = keep.tile([P, T], U8, name="out_sc", align_bytes=64)
         out_words = out_1[0].rearrange("p t i -> p (t i)").bitcast(I32)
-        for a in range(out_tiles):
-            cols = slice(a * OUT_COLS, (a + 1) * OUT_COLS)
-            out_codes = keep.tile([P, OUT_COLS], I32, name=f"out_codes{a}", align_bytes=64)
-            nc.vector.quantize_mx(out_codes[:].bitcast(FP8X4), out_sc[:, cols], out_bf[a][:].rearrange("p c t -> p (c t)"))
-            nc.sync.dma_start(out_words[:, cols], out_codes[:])
+        for a in (1, 0, 2):
+            s = spans[a]
+            out_codes = keep.tile([P, s.stop - s.start], I32, name=f"out_codes{a}", align_bytes=64)
+            nc.vector.quantize_mx(out_codes[:].bitcast(FP8X4), out_sc[:, s], out_bf[a][:].rearrange("p c t -> p (c t)"))
+            nc.sync.dma_start(out_words[:, s], out_codes[:])
         for q in range(4):
             nc.scalar.dma_start(out_2[0, 4 * q : 4 * q + 4, :].bitcast(I32), out_sc[32 * q : 32 * q + 4, :].bitcast(I32))

@@ -20,8 +20,7 @@ P = 128
 PACK = 4
 HALF = 512
 CHUNK = 128
-EARLY_PAGES = 1
-LEAD = 3
+PIECE = 256
 
 
 def tile_list_modp_ggelu_gateP_kernel(
@@ -32,78 +31,67 @@ def tile_list_modp_ggelu_gateP_kernel(
     chunks = HALF // CHUNK
     with ExitStack() as ctx:
         keep = ctx.enter_context(tc.tile_pool(name="keep", bufs=1))
-        ring = ctx.enter_context(tc.tile_pool(name="ring", bufs=2))
         psum = ctx.enter_context(tc.psum_pool(name="psum", bufs=1))
-        psum_y = ctx.enter_context(tc.psum_pool(name="psum_y", bufs=2))
 
         offsets = keep.tile([P, J // 16], U16, name="offsets")
         nc.sync.dma_start(offsets[:], offs)
 
-        def listed(h):
-            return offsets[:, h * HALF // 16 : (h + 1) * HALF // 16]
-
-        tab_plane = keep.tile([P, T], U8, name="tab_plane", tag="gate0", align_bytes=64)
-        wg_plane = keep.tile([P, R], U8, name="wg_plane", tag="wd_raw", align_bytes=64)
+        tab_plane = keep.tile([P, T], U8, name="tab_plane", align_bytes=64)
+        wg_plane = keep.tile([P, R], U8, name="wg_plane", align_bytes=64)
         nc.gpsimd.memset(tab_plane[:].bitcast(I32), 0)
         nc.gpsimd.memset(wg_plane[:].bitcast(I32), 0)
         warm = keep.tile([P, 1], F32, name="warm")
         warm_out = keep.tile([P, 1], F32, name="warm_out")
         nc.vector.memset(warm[:], 0.0)
         nc.scalar.activation(warm_out[:], warm[:], GELU)
+        pages = []
 
-        wg_raw = keep.tile([P, R // 2], I32, name="wg_raw", tag="wgo", align_bytes=64)
-        nc.sync.dma_start(wg_raw[:], wg_words[0].bitcast(I32))
-        for q in range(4):
-            nc.sync.dma_start(tab_plane[32 * q : 32 * q + 4, :].bitcast(I32), tab_scales[0, 4 * q : 4 * q + 4, :].bitcast(I32))
-        tab_codes = keep.tile([P, T], I32, name="tab_codes", tag="gate1", align_bytes=64)
-        nc.sync.dma_start(tab_codes[:], tab_words[0].rearrange("p t i -> p (t i)").bitcast(I32))
         wu_rows = wu.rearrange("(p j) c -> p j c", j=PACK)
-        wu_lo = keep.tile([P, PACK, R // 2], F32, name="wu_lo", tag="gate3", align_bytes=64)
+        wu_lo = keep.tile([P, PACK, R // 2], F32, name="wu_lo", align_bytes=64)
         nc.sync.dma_start(wu_lo[:], wu_rows[:, :, : R // 2])
         for q in range(4):
-            nc.sync.dma_start(wg_plane[32 * q : 32 * q + 4, :].bitcast(I32), wg_scales[0, 4 * q : 4 * q + 4, :].bitcast(I32))
-        wu_hi = keep.tile([P, PACK, R // 2], F32, name="wu_hi", tag="gate2", align_bytes=64)
+            nc.sync.dma_start(tab_plane[32 * q : 32 * q + 4, :].bitcast(I32), tab_scales[0, 4 * q : 4 * q + 4, :].bitcast(I32))
+        wg_raw = keep.tile([P, R // 2], I32, name="wg_raw", align_bytes=64)
+        nc.sync.dma_start(wg_raw[:], wg_words[0].bitcast(I32))
+        wu_hi = keep.tile([P, PACK, R // 2], F32, name="wu_hi", align_bytes=64)
         nc.sync.dma_start(wu_hi[:], wu_rows[:, :, R // 2 :])
+        tab_codes = keep.tile([P, T], I32, name="tab_codes", align_bytes=64)
+        nc.sync.dma_start(tab_codes[:], tab_words[0].rearrange("p t i -> p (t i)").bitcast(I32))
+        for q in range(4):
+            nc.sync.dma_start(wg_plane[32 * q : 32 * q + 4, :].bitcast(I32), wg_scales[0, 4 * q : 4 * q + 4, :].bitcast(I32))
 
-        pages = []
-        for t in range(EARLY_PAGES):
-            page = keep.tile([P, T], F32, name="page", tag=f"page{t}")
-            nc.vector.memset(page[:].bitcast(I32), 0)
-            pages.append(page)
+        v_sc = keep.tile([P, J], U8, name="v_sc", align_bytes=64)
+        nc.vector.tensor_copy(v_sc[:], tab_plane[:].indirect(offsets[:]))
 
         wg_codes = keep.tile([P, 2 * R], U8, name="wg_codes", align_bytes=64)
         wg_sc = keep.tile([P, R], U8, name="wg_sc", align_bytes=64)
         nc.vector.tensor_copy(
-            wg_codes[:].bitcast(I32).rearrange("p (t m u) -> p t m u", t=PACK, u=2),
-            wg_raw[:].rearrange("p (m t u) -> p t m u", t=PACK, u=2),
+            wg_codes[:].bitcast(U16).rearrange("p (t m) -> p t m", t=PACK),
+            wg_raw[:].bitcast(U16).rearrange("p (m t) -> p t m", t=PACK),
         )
-        wgo_sb = keep.tile([P, J], F32, name="wgo_sb", tag="wgo", align_bytes=64)
-        nc.sync.dma_start(wgo_sb[:], wgo)
-
-        v_sc = keep.tile([P, J], U8, name="v_sc", align_bytes=64)
-        nc.vector.tensor_copy(v_sc[:], tab_plane[:].indirect(offsets[:]))
-        v_codes = []
-        for h in range(halves):
-            codes = keep.tile([P, HALF], U32, name=f"v_codes{h}", align_bytes=64)
-            nc.vector.tensor_copy(codes[:], tab_codes[:].bitcast(U32).indirect(listed(h)))
-            v_codes.append(codes)
-            if h == 0:
-                nc.vector.tensor_copy(
-                    wg_sc[:].bitcast(I32).rearrange("p (t m) -> p t m", t=PACK),
-                    wg_plane[:].bitcast(I32).rearrange("p (m t) -> p t m", t=PACK),
-                )
-        wd_raw = keep.tile([P, PACK, N], F32, name="wd_raw", tag="wd_raw", align_bytes=64)
-        wd_rows = wd.rearrange("(m s i) n -> i m s n", s=PACK, i=4)
-        for i in range(4):
-            nc.sync.dma_start(wd_raw[i:P:4, :, :], wd_rows[i])
+        nc.vector.tensor_copy(
+            wg_sc[:].rearrange("p (t m) -> p t m", t=PACK),
+            wg_plane[:].rearrange("p (m t) -> p t m", t=PACK),
+        )
 
         wu_bf = keep.tile([P, PACK * R], BF16, name="wu_bf", align_bytes=64)
-        wu_dealt = wu_bf[:].rearrange("p (t m i j) -> p m t j i", t=PACK, i=4, j=PACK)
-        nc.scalar.copy(wu_dealt[:, :16], wu_lo[:].rearrange("p j (m t i) -> p m t j i", t=PACK, i=4))
-        nc.vector.tensor_copy(wu_dealt[:, 16:], wu_hi[:].rearrange("p j (m t i) -> p m t j i", t=PACK, i=4))
+        wu_dealt = wu_bf[:].rearrange("p (t m j) -> p m j t", t=PACK, j=PACK)
+        nc.scalar.copy(wu_dealt[:, : P // 2], wu_lo[:].rearrange("p j (m t) -> p m j t", t=PACK))
+        nc.scalar.copy(wu_dealt[:, P // 2 :], wu_hi[:].rearrange("p j (m t) -> p m j t", t=PACK))
         wu_codes = keep.tile([P, R], U32, name="wu_codes", align_bytes=64)
         wu_sc = keep.tile([P, R], U8, name="wu_sc", align_bytes=64)
         nc.vector.quantize_mx(wu_codes[:].bitcast(FP8X4), wu_sc[:], wu_bf[:])
+
+        v_codes = []
+        for g in range(J // PIECE):
+            codes = keep.tile([P, PIECE], U32, name=f"v_codes{g}", align_bytes=64)
+            nc.vector.tensor_copy(codes[:], tab_codes[:].bitcast(U32).indirect(offsets[:, g * PIECE // 16 : (g + 1) * PIECE // 16]))
+            v_codes.append(codes)
+
+        wd_raw = keep.tile([P, PACK, N], F32, name="wd_raw", tag="wd_raw", align_bytes=64)
+        nc.sync.dma_start(wd_raw[:], wd.rearrange("(p s) n -> p s n", s=PACK))
+        wgo_sb = keep.tile([P, J], F32, name="wgo_sb", tag="wgo", align_bytes=64)
+        nc.sync.dma_start(wgo_sb[:], wgo)
 
         wd_sc = keep.tile([P, N], U8, name="wd_sc", align_bytes=64)
 
@@ -114,8 +102,8 @@ def tile_list_modp_ggelu_gateP_kernel(
             nc.sync.dma_start(gate[:], gT_rows[t])
             gates.append(gate)
 
-        def weighted_gate(t):
-            gw = ring.tile([P, J], F32, name="gw")
+        def weighted_gate(t, tag):
+            gw = keep.tile([P, J], F32, name="gw", tag=tag, align_bytes=64)
             nc.vector.tensor_tensor(gw[:], gates[t][:].indirect(offsets[:]), wgo_sb[:], MULT)
             return gw
 
@@ -124,42 +112,42 @@ def tile_list_modp_ggelu_gateP_kernel(
             nc.gpsimd.memset(page[:], 0.0)
             pages.append(page)
 
+        def product(n, bank, w_codes, w_dtype, width, w_sc):
+            acc = psum.tile([P, PACK, CHUNK], F32, name="acc", tag=bank)
+            piece = v_codes[n * CHUNK // PIECE]
+            first = n * CHUNK % PIECE
+            for t in range(PACK):
+                nc.tensor.matmul_mx(
+                    acc[:, t, :],
+                    lhsT=w_codes[:, width * t : width * (t + 1)].bitcast(w_dtype),
+                    lhsT_scale=w_sc[:, P * t : P * (t + 1)],
+                    rhs=piece[:, first : first + CHUNK].bitcast(FP8X4),
+                    rhs_scale=v_sc[:, n * CHUNK : (n + 1) * CHUNK],
+                    start=True,
+                    stop=True,
+                )
+            return acc
+
+        def gelu_chunk(n):
+            ga = product(n, f"ga{n % 4}", wg_codes, FP4X4, 2 * P, wg_sc)
+            act = keep.tile([P, CHUNK, PACK], F32, name="act", tag=f"act{n}", align_bytes=64)
+            nc.scalar.activation(act[:], ga[:].rearrange("p t j -> p j t"), GELU)
+            return act
+
         gws = []
         h_codes, h_sc = [], []
+        acts = [gelu_chunk(0)]
         for h in range(halves):
             h_bf = keep.tile([P, PACK * HALF], BF16, name=f"h_bf{h}", align_bytes=64)
             for c in range(chunks):
-                cols = slice(c * CHUNK, (c + 1) * CHUNK)
                 n = h * chunks + c
-                turn = (n // LEAD) % 2
-                ga = psum.tile([P, PACK, CHUNK], F32, name="ga", tag=f"bank{turn}_{n % LEAD}")
-                for t in range(PACK):
-                    nc.tensor.matmul_mx(
-                        ga[:, t, :],
-                        lhsT=wg_codes[:, 2 * P * t : 2 * P * (t + 1)].bitcast(FP4X4),
-                        lhsT_scale=wg_sc[:, P * t : P * (t + 1)],
-                        rhs=v_codes[h][:, cols].bitcast(FP8X4),
-                        rhs_scale=v_sc[:, h * HALF + c * CHUNK : h * HALF + (c + 1) * CHUNK],
-                        start=True,
-                        stop=True,
-                    )
-                ub = psum.tile([P, PACK, CHUNK], F32, name="ub", tag=f"bank{1 - turn}_{n % LEAD}")
-                for t in range(PACK):
-                    nc.tensor.matmul_mx(
-                        ub[:, t, :],
-                        lhsT=wu_codes[:, P * t : P * (t + 1)].bitcast(FP8X4),
-                        lhsT_scale=wu_sc[:, P * t : P * (t + 1)],
-                        rhs=v_codes[h][:, cols].bitcast(FP8X4),
-                        rhs_scale=v_sc[:, h * HALF + c * CHUNK : h * HALF + (c + 1) * CHUNK],
-                        start=True,
-                        stop=True,
-                    )
-                act = keep.tile([P, CHUNK, PACK], F32, name="act", tag=f"act{n}", align_bytes=64)
-                nc.scalar.activation(act[:], ga[:].rearrange("p t j -> p j t"), GELU)
+                if n + 1 < halves * chunks:
+                    acts.append(gelu_chunk(n + 1))
+                ub = product(n, f"ub{n % 4}", wu_codes, FP8X4, P, wu_sc)
                 nc.vector.tensor_tensor(
                     h_bf[:, PACK * c * CHUNK : PACK * (c + 1) * CHUNK].rearrange("p (j t) -> p j t", t=PACK),
                     ub[:].rearrange("p t j -> p j t"),
-                    act[:],
+                    acts[n][:],
                     MULT,
                 )
             codes = keep.tile([P, HALF], U32, name=f"h_codes{h}", align_bytes=64)
@@ -168,21 +156,21 @@ def tile_list_modp_ggelu_gateP_kernel(
             h_codes.append(codes)
             h_sc.append(sc)
 
-        wd_bf = keep.tile([P, PACK * N], BF16, name="wd_bf", tag=f"act{chunks}", align_bytes=64)
-        nc.scalar.copy(
-            wd_bf[:].rearrange("p (t m s) -> p m s t", t=PACK, s=PACK),
-            wd_raw[:].rearrange("p s (m t) -> p m s t", t=PACK),
-        )
-
-        gws.append(weighted_gate(0))
-        wd_codes = keep.tile([P, N], U32, name="wd_codes", tag="gate0", align_bytes=64)
-        nc.vector.quantize_mx(wd_codes[:].bitcast(FP8X4), wd_sc[:], wd_bf[:])
-        late_page(f"act{chunks}")
+        wd_codes = keep.tile([P, N], U32, name="wd_codes", align_bytes=64)
+        wd_src = wd_raw[:].rearrange("p s (m t) -> p m s t", t=PACK)
+        for u, tag in enumerate(["wd_bf", "act5"]):
+            bf = keep.tile([P, 2 * N], BF16, name="wd_bf", tag=tag, align_bytes=64)
+            nc.scalar.copy(bf[:].rearrange("p (t m s) -> p m s t", t=2, s=PACK), wd_src[:, :, :, 2 * u : 2 * u + 2])
+            cols = slice(u * N // 2, (u + 1) * N // 2)
+            nc.vector.quantize_mx(wd_codes[:, cols].bitcast(FP8X4), wd_sc[:, cols], bf[:])
+        gws.append(weighted_gate(0, "act5"))
+        late_page("gate0")
         ys = []
+        y_banks = ["ga0", "ga1", "ga2", "ga3", "ub0", "ub1", "ub2", "ub3"]
         for t in range(PACK):
             y = keep.tile([P, J], F32, name=f"y{t}")
             for h in range(halves):
-                y_ps = psum_y.tile([P, HALF], F32, name="y_ps")
+                y_ps = psum.tile([P, HALF], F32, name="y_ps", tag=y_banks[t * halves + h])
                 nc.tensor.matmul_mx(
                     y_ps[:],
                     lhsT=wd_codes[:, P * t : P * (t + 1)].bitcast(FP8X4),
@@ -200,8 +188,7 @@ def tile_list_modp_ggelu_gateP_kernel(
         out_rows = out_0.rearrange("(p t) c -> t p c", t=PACK)
         for t in range(PACK):
             if t + 1 < PACK:
-                gws.append(weighted_gate(t + 1))
-            if t + 2 < PACK:
+                gws.append(weighted_gate(t + 1, f"gw{t + 1}"))
                 late_page(f"gate{t + 1}")
             nc.vector.tensor_tensor(pages[t][:].indirect(offsets[:]), ys[t][:], gws[t][:], MULT)
             nc.sync.dma_start(out_rows[t], pages[t][:])

@@ -38,13 +38,17 @@ def tile_list_modp_ggelu_gateP_kernel(
 
         tab_plane = keep.tile([P, T], U8, name="tab_plane", align_bytes=64)
         wg_plane = keep.tile([P, R], U8, name="wg_plane", align_bytes=64)
-        nc.gpsimd.memset(tab_plane[:].bitcast(I32), 0)
-        nc.gpsimd.memset(wg_plane[:].bitcast(I32), 0)
+        nc.vector.memset(tab_plane[:].bitcast(I32), 0)
+        nc.vector.memset(wg_plane[:].bitcast(I32), 0)
         warm = keep.tile([P, 1], F32, name="warm")
         warm_out = keep.tile([P, 1], F32, name="warm_out")
         nc.vector.memset(warm[:], 0.0)
         nc.scalar.activation(warm_out[:], warm[:], GELU)
         pages = []
+        for t in range(PACK - 1):
+            page = keep.tile([P, T], F32, name="page", tag=f"page{t}")
+            nc.vector.memset(page[:].bitcast(I32), 0)
+            pages.append(page)
 
         wu_rows = wu.rearrange("(p j) c -> p j c", j=PACK)
         wu_lo = keep.tile([P, PACK, R // 2], F32, name="wu_lo", align_bytes=64)
@@ -55,7 +59,7 @@ def tile_list_modp_ggelu_gateP_kernel(
         nc.sync.dma_start(wg_raw[:], wg_words[0].bitcast(I32))
         wu_hi = keep.tile([P, PACK, R // 2], F32, name="wu_hi", align_bytes=64)
         nc.sync.dma_start(wu_hi[:], wu_rows[:, :, R // 2 :])
-        tab_codes = keep.tile([P, T], I32, name="tab_codes", align_bytes=64)
+        tab_codes = keep.tile([P, T], I32, name="tab_codes", tag="page3", align_bytes=64)
         nc.sync.dma_start(tab_codes[:], tab_words[0].rearrange("p t i -> p (t i)").bitcast(I32))
         for q in range(4):
             nc.sync.dma_start(wg_plane[32 * q : 32 * q + 4, :].bitcast(I32), wg_scales[0, 4 * q : 4 * q + 4, :].bitcast(I32))
@@ -134,11 +138,12 @@ def tile_list_modp_ggelu_gateP_kernel(
             nc.scalar.activation(act[:], ga[:].rearrange("p t j -> p j t"), GELU)
             return act
 
+        late_page("page3")
         gws = []
         h_codes, h_sc = [], []
         acts = [gelu_chunk(0)]
         for h in range(halves):
-            h_bf = keep.tile([P, PACK * HALF], BF16, name=f"h_bf{h}", align_bytes=64)
+            h_bf = keep.tile([P, PACK * HALF], BF16, name="h_bf", tag=f"h_bf{h}", align_bytes=64)
             for c in range(chunks):
                 n = h * chunks + c
                 if n + 1 < halves * chunks:
@@ -157,14 +162,13 @@ def tile_list_modp_ggelu_gateP_kernel(
             h_sc.append(sc)
 
         wd_codes = keep.tile([P, N], U32, name="wd_codes", align_bytes=64)
-        wd_src = wd_raw[:].rearrange("p s (m t) -> p m s t", t=PACK)
-        for u, tag in enumerate(["wd_bf", "act5"]):
-            bf = keep.tile([P, 2 * N], BF16, name="wd_bf", tag=tag, align_bytes=64)
-            nc.scalar.copy(bf[:].rearrange("p (t m s) -> p m s t", t=2, s=PACK), wd_src[:, :, :, 2 * u : 2 * u + 2])
-            cols = slice(u * N // 2, (u + 1) * N // 2)
-            nc.vector.quantize_mx(wd_codes[:, cols].bitcast(FP8X4), wd_sc[:, cols], bf[:])
-        gws.append(weighted_gate(0, "act5"))
-        late_page("gate0")
+        wd_bf = keep.tile([P, PACK * N], BF16, name="wd_bf", tag="act5", align_bytes=64)
+        nc.scalar.copy(
+            wd_bf[:].rearrange("p (t m s) -> p m s t", t=PACK, s=PACK),
+            wd_raw[:].rearrange("p s (m t) -> p m s t", t=PACK),
+        )
+        gws.append(weighted_gate(0, "gw0"))
+        nc.vector.quantize_mx(wd_codes[:].bitcast(FP8X4), wd_sc[:], wd_bf[:])
         ys = []
         y_banks = ["ga0", "ga1", "ga2", "ga3", "ub0", "ub1", "ub2", "ub3"]
         for t in range(PACK):
@@ -188,8 +192,7 @@ def tile_list_modp_ggelu_gateP_kernel(
         out_rows = out_0.rearrange("(p t) c -> t p c", t=PACK)
         for t in range(PACK):
             if t + 1 < PACK:
-                gws.append(weighted_gate(t + 1, f"gw{t + 1}"))
-                late_page(f"gate{t + 1}")
+                gws.append(weighted_gate(t + 1, ["act5", "gw2", "gw3"][t]))
             nc.vector.tensor_tensor(pages[t][:].indirect(offsets[:]), ys[t][:], gws[t][:], MULT)
             nc.sync.dma_start(out_rows[t], pages[t][:])
             for a, s in enumerate(spans):

@@ -38,16 +38,16 @@ def tile_list_modp_ggelu_gateP_kernel(
 
         tab_plane = keep.tile([P, T], U8, name="tab_plane", align_bytes=64)
         wg_plane = keep.tile([P, R], U8, name="wg_plane", align_bytes=64)
-        nc.vector.memset(tab_plane[:].bitcast(I32), 0)
-        nc.vector.memset(wg_plane[:].bitcast(I32), 0)
+        nc.gpsimd.memset(tab_plane[:].bitcast(I32), 0)
+        nc.gpsimd.memset(wg_plane[:].bitcast(I32), 0)
         warm = keep.tile([P, 1], F32, name="warm")
         warm_out = keep.tile([P, 1], F32, name="warm_out")
         nc.vector.memset(warm[:], 0.0)
         nc.scalar.activation(warm_out[:], warm[:], GELU)
         pages = []
-        for t in range(PACK - 1):
+        for t in range(2):
             page = keep.tile([P, T], F32, name="page", tag=f"page{t}")
-            nc.vector.memset(page[:].bitcast(I32), 0)
+            nc.gpsimd.memset(page[:], 0.0)
             pages.append(page)
 
         wu_rows = wu.rearrange("(p j) c -> p j c", j=PACK)
@@ -59,7 +59,7 @@ def tile_list_modp_ggelu_gateP_kernel(
         nc.sync.dma_start(wg_raw[:], wg_words[0].bitcast(I32))
         wu_hi = keep.tile([P, PACK, R // 2], F32, name="wu_hi", align_bytes=64)
         nc.sync.dma_start(wu_hi[:], wu_rows[:, :, R // 2 :])
-        tab_codes = keep.tile([P, T], I32, name="tab_codes", tag="page3", align_bytes=64)
+        tab_codes = keep.tile([P, T], I32, name="tab_codes", tag="page2", align_bytes=64)
         nc.sync.dma_start(tab_codes[:], tab_words[0].rearrange("p t i -> p (t i)").bitcast(I32))
         for q in range(4):
             nc.sync.dma_start(wg_plane[32 * q : 32 * q + 4, :].bitcast(I32), wg_scales[0, 4 * q : 4 * q + 4, :].bitcast(I32))
@@ -92,8 +92,6 @@ def tile_list_modp_ggelu_gateP_kernel(
             nc.vector.tensor_copy(codes[:], tab_codes[:].bitcast(U32).indirect(offsets[:, g * PIECE // 16 : (g + 1) * PIECE // 16]))
             v_codes.append(codes)
 
-        wd_raw = keep.tile([P, PACK, N], F32, name="wd_raw", tag="wd_raw", align_bytes=64)
-        nc.sync.dma_start(wd_raw[:], wd.rearrange("(p s) n -> p s n", s=PACK))
         wgo_sb = keep.tile([P, J], F32, name="wgo_sb", tag="wgo", align_bytes=64)
         nc.sync.dma_start(wgo_sb[:], wgo)
 
@@ -105,6 +103,9 @@ def tile_list_modp_ggelu_gateP_kernel(
             gate = keep.tile([P, T], F32, name="gate", tag=f"gate{t}", align_bytes=64)
             nc.sync.dma_start(gate[:], gT_rows[t])
             gates.append(gate)
+            if t == 0:
+                wd_raw = keep.tile([P, PACK, N], F32, name="wd_raw", align_bytes=64)
+                nc.sync.dma_start(wd_raw[:], wd.rearrange("(p s) n -> p s n", s=PACK))
 
         def weighted_gate(t, tag):
             gw = keep.tile([P, J], F32, name="gw", tag=tag, align_bytes=64)
@@ -138,12 +139,22 @@ def tile_list_modp_ggelu_gateP_kernel(
             nc.scalar.activation(act[:], ga[:].rearrange("p t j -> p j t"), GELU)
             return act
 
-        late_page("page3")
+        late_page("page2")
         gws = []
         h_codes, h_sc = [], []
+        h_bfs = []
+
+        def quantise_h(h):
+            codes = keep.tile([P, HALF], U32, name=f"h_codes{h}", align_bytes=64)
+            sc = keep.tile([P, HALF], U8, name=f"h_sc{h}", align_bytes=64)
+            nc.vector.quantize_mx(codes[:].bitcast(FP8X4), sc[:], h_bfs[h][:])
+            h_codes.append(codes)
+            h_sc.append(sc)
+
         acts = [gelu_chunk(0)]
         for h in range(halves):
             h_bf = keep.tile([P, PACK * HALF], BF16, name="h_bf", tag=f"h_bf{h}", align_bytes=64)
+            h_bfs.append(h_bf)
             for c in range(chunks):
                 n = h * chunks + c
                 if n + 1 < halves * chunks:
@@ -155,11 +166,11 @@ def tile_list_modp_ggelu_gateP_kernel(
                     acts[n][:],
                     MULT,
                 )
-            codes = keep.tile([P, HALF], U32, name=f"h_codes{h}", align_bytes=64)
-            sc = keep.tile([P, HALF], U8, name=f"h_sc{h}", align_bytes=64)
-            nc.vector.quantize_mx(codes[:].bitcast(FP8X4), sc[:], h_bf[:])
-            h_codes.append(codes)
-            h_sc.append(sc)
+                if n == chunks:
+                    quantise_h(0)
+        gws.append(weighted_gate(0, "gw0"))
+        gws.append(weighted_gate(1, "act7"))
+        quantise_h(1)
 
         wd_codes = keep.tile([P, N], U32, name="wd_codes", align_bytes=64)
         wd_bf = keep.tile([P, PACK * N], BF16, name="wd_bf", tag="act5", align_bytes=64)
@@ -167,8 +178,9 @@ def tile_list_modp_ggelu_gateP_kernel(
             wd_bf[:].rearrange("p (t m s) -> p m s t", t=PACK, s=PACK),
             wd_raw[:].rearrange("p s (m t) -> p m s t", t=PACK),
         )
-        gws.append(weighted_gate(0, "gw0"))
         nc.vector.quantize_mx(wd_codes[:].bitcast(FP8X4), wd_sc[:], wd_bf[:])
+        gws.append(weighted_gate(2, "act5"))
+        late_page("gate2")
         ys = []
         y_banks = ["ga0", "ga1", "ga2", "ga3", "ub0", "ub1", "ub2", "ub3"]
         for t in range(PACK):
@@ -187,29 +199,30 @@ def tile_list_modp_ggelu_gateP_kernel(
                 nc.scalar.copy(y[:, h * HALF : (h + 1) * HALF], y_ps[:])
             ys.append(y)
 
-        spans = [slice(0, T // 2), slice(T // 2, 3 * T // 4), slice(3 * T // 4, T)]
+        edges = [0, 512, 1024, 1536, 1792, 2048]
+        spans = [slice(lo, hi) for lo, hi in zip(edges, edges[1:])]
         out_bf = [keep.tile([P, s.stop - s.start, PACK], BF16, name=f"out_bf{a}", align_bytes=64) for a, s in enumerate(spans)]
         out_rows = out_0.rearrange("(p t) c -> t p c", t=PACK)
         for t in range(PACK):
-            if t + 1 < PACK:
-                gws.append(weighted_gate(t + 1, ["act5", "gw2", "gw3"][t]))
+            if t == 2:
+                gws.append(weighted_gate(3, "act7"))
             nc.vector.tensor_tensor(pages[t][:].indirect(offsets[:]), ys[t][:], gws[t][:], MULT)
             nc.sync.dma_start(out_rows[t], pages[t][:])
             for a, s in enumerate(spans):
                 src = pages[t][:, s]
-                if a == 0 and t == PACK - 1:
+                if a < 2 and t == PACK - 1:
                     nc.vector.tensor_copy(out_bf[a][:, :, t], src)
-                elif a == 0 and t == PACK - 2:
-                    nc.scalar.copy(out_bf[a][:, :, t : t + 2], src.unsqueeze(2).to_broadcast([P, T // 2, 2]))
+                elif a < 2 and t == PACK - 2:
+                    nc.scalar.copy(out_bf[a][:, :, t : t + 2], src.unsqueeze(2).to_broadcast([P, s.stop - s.start, 2]))
                 else:
                     nc.scalar.copy(out_bf[a][:, :, t], src)
 
         out_sc = keep.tile([P, T], U8, name="out_sc", align_bytes=64)
         out_words = out_1[0].rearrange("p t i -> p (t i)").bitcast(I32)
-        for a in (1, 0, 2):
-            s = spans[a]
+        for a, s in enumerate(spans):
             out_codes = keep.tile([P, s.stop - s.start], I32, name=f"out_codes{a}", align_bytes=64)
             nc.vector.quantize_mx(out_codes[:].bitcast(FP8X4), out_sc[:, s], out_bf[a][:].rearrange("p c t -> p (c t)"))
             nc.sync.dma_start(out_words[:, s], out_codes[:])
         for q in range(4):
-            nc.scalar.dma_start(out_2[0, 4 * q : 4 * q + 4, :].bitcast(I32), out_sc[32 * q : 32 * q + 4, :].bitcast(I32))
+            queue = nc.scalar if q % 2 == 0 else nc.sync
+            queue.dma_start(out_2[0, 4 * q : 4 * q + 4, :].bitcast(I32), out_sc[32 * q : 32 * q + 4, :].bitcast(I32))

@@ -28,7 +28,6 @@ def tile_list_modp_ggelu_gateP_kernel(
 ):
     nc = tc.nc
     halves = J // HALF
-    chunks = HALF // CHUNK
     with ExitStack() as ctx:
         keep = ctx.enter_context(tc.tile_pool(name="keep", bufs=1))
         psum = ctx.enter_context(tc.psum_pool(name="psum", bufs=1))
@@ -47,7 +46,7 @@ def tile_list_modp_ggelu_gateP_kernel(
         pages = []
         for t in range(2):
             page = keep.tile([P, T], F32, name="page", tag=f"page{t}")
-            nc.gpsimd.memset(page[:], 0.0)
+            nc.vector.memset(page[:].bitcast(I32), 0)
             pages.append(page)
 
         wu_rows = wu.rearrange("(p j) c -> p j c", j=PACK)
@@ -92,6 +91,8 @@ def tile_list_modp_ggelu_gateP_kernel(
             nc.vector.tensor_copy(codes[:], tab_codes[:].bitcast(U32).indirect(offsets[:, g * PIECE // 16 : (g + 1) * PIECE // 16]))
             v_codes.append(codes)
 
+        wd_raw = keep.tile([P, PACK, N], F32, name="wd_raw", align_bytes=64)
+        nc.sync.dma_start(wd_raw[:], wd.rearrange("(p s) n -> p s n", s=PACK))
         wgo_sb = keep.tile([P, J], F32, name="wgo_sb", tag="wgo", align_bytes=64)
         nc.sync.dma_start(wgo_sb[:], wgo)
 
@@ -103,9 +104,6 @@ def tile_list_modp_ggelu_gateP_kernel(
             gate = keep.tile([P, T], F32, name="gate", tag=f"gate{t}", align_bytes=64)
             nc.sync.dma_start(gate[:], gT_rows[t])
             gates.append(gate)
-            if t == 0:
-                wd_raw = keep.tile([P, PACK, N], F32, name="wd_raw", align_bytes=64)
-                nc.sync.dma_start(wd_raw[:], wd.rearrange("(p s) n -> p s n", s=PACK))
 
         def weighted_gate(t, tag):
             gw = keep.tile([P, J], F32, name="gw", tag=tag, align_bytes=64)
@@ -141,36 +139,24 @@ def tile_list_modp_ggelu_gateP_kernel(
 
         late_page("page2")
         gws = []
-        h_codes, h_sc = [], []
-        h_bfs = []
-
-        def quantise_h(h):
-            codes = keep.tile([P, HALF], U32, name=f"h_codes{h}", align_bytes=64)
-            sc = keep.tile([P, HALF], U8, name=f"h_sc{h}", align_bytes=64)
-            nc.vector.quantize_mx(codes[:].bitcast(FP8X4), sc[:], h_bfs[h][:])
-            h_codes.append(codes)
-            h_sc.append(sc)
-
+        h_bf = keep.tile([P, PACK * J], BF16, name="h_bf", align_bytes=64)
         acts = [gelu_chunk(0)]
-        for h in range(halves):
-            h_bf = keep.tile([P, PACK * HALF], BF16, name="h_bf", tag=f"h_bf{h}", align_bytes=64)
-            h_bfs.append(h_bf)
-            for c in range(chunks):
-                n = h * chunks + c
-                if n + 1 < halves * chunks:
-                    acts.append(gelu_chunk(n + 1))
-                ub = product(n, f"ub{n % 4}", wu_codes, FP8X4, P, wu_sc)
-                nc.vector.tensor_tensor(
-                    h_bf[:, PACK * c * CHUNK : PACK * (c + 1) * CHUNK].rearrange("p (j t) -> p j t", t=PACK),
-                    ub[:].rearrange("p t j -> p j t"),
-                    acts[n][:],
-                    MULT,
-                )
-                if n == chunks:
-                    quantise_h(0)
-        gws.append(weighted_gate(0, "gw0"))
-        gws.append(weighted_gate(1, "act7"))
-        quantise_h(1)
+        for n in range(J // CHUNK):
+            if n + 1 < J // CHUNK:
+                acts.append(gelu_chunk(n + 1))
+            ub = product(n, f"ub{n % 4}", wu_codes, FP8X4, P, wu_sc)
+            nc.vector.tensor_tensor(
+                h_bf[:, PACK * n * CHUNK : PACK * (n + 1) * CHUNK].rearrange("p (j t) -> p j t", t=PACK),
+                ub[:].rearrange("p t j -> p j t"),
+                acts[n][:],
+                MULT,
+            )
+            if n == 0:
+                late_page("act0")
+        gws.append(weighted_gate(0, "act7"))
+        h_codes = keep.tile([P, J], U32, name="h_codes", align_bytes=64)
+        h_sc = keep.tile([P, J], U8, name="h_sc", align_bytes=64)
+        nc.vector.quantize_mx(h_codes[:].bitcast(FP8X4), h_sc[:], h_bf[:])
 
         wd_codes = keep.tile([P, N], U32, name="wd_codes", align_bytes=64)
         wd_bf = keep.tile([P, PACK * N], BF16, name="wd_bf", tag="act5", align_bytes=64)
@@ -179,8 +165,6 @@ def tile_list_modp_ggelu_gateP_kernel(
             wd_raw[:].rearrange("p s (m t) -> p m s t", t=PACK),
         )
         nc.vector.quantize_mx(wd_codes[:].bitcast(FP8X4), wd_sc[:], wd_bf[:])
-        gws.append(weighted_gate(2, "act5"))
-        late_page("gate2")
         ys = []
         y_banks = ["ga0", "ga1", "ga2", "ga3", "ub0", "ub1", "ub2", "ub3"]
         for t in range(PACK):
@@ -191,8 +175,8 @@ def tile_list_modp_ggelu_gateP_kernel(
                     y_ps[:],
                     lhsT=wd_codes[:, P * t : P * (t + 1)].bitcast(FP8X4),
                     lhsT_scale=wd_sc[:, P * t : P * (t + 1)],
-                    rhs=h_codes[h][:].bitcast(FP8X4),
-                    rhs_scale=h_sc[h][:],
+                    rhs=h_codes[:, h * HALF : (h + 1) * HALF].bitcast(FP8X4),
+                    rhs_scale=h_sc[:, h * HALF : (h + 1) * HALF],
                     start=True,
                     stop=True,
                 )
@@ -204,8 +188,8 @@ def tile_list_modp_ggelu_gateP_kernel(
         out_bf = [keep.tile([P, s.stop - s.start, PACK], BF16, name=f"out_bf{a}", align_bytes=64) for a, s in enumerate(spans)]
         out_rows = out_0.rearrange("(p t) c -> t p c", t=PACK)
         for t in range(PACK):
-            if t == 2:
-                gws.append(weighted_gate(3, "act7"))
+            if t + 1 < PACK:
+                gws.append(weighted_gate(t + 1, ["act5", "act7", "act5"][t]))
             nc.vector.tensor_tensor(pages[t][:].indirect(offsets[:]), ys[t][:], gws[t][:], MULT)
             nc.sync.dma_start(out_rows[t], pages[t][:])
             for a, s in enumerate(spans):

@@ -36,9 +36,9 @@ def tile_list_modp_ggelu_gateP_kernel(
         nc.sync.dma_start(offsets[:], offs)
 
         tab_plane = keep.tile([P, T], U8, name="tab_plane", align_bytes=64)
-        wg_plane = keep.tile([P, R], U8, name="wg_plane", align_bytes=64)
-        nc.gpsimd.memset(tab_plane[:].bitcast(I32), 0)
-        nc.gpsimd.memset(wg_plane[:].bitcast(I32), 0)
+        wg_plane = keep.tile([P, R], U8, name="wg_plane", tag="v_codes1", align_bytes=64)
+        nc.vector.memset(tab_plane[:].bitcast(I32), 0)
+        nc.vector.memset(wg_plane[:].bitcast(I32), 0)
         warm = keep.tile([P, 1], F32, name="warm")
         warm_out = keep.tile([P, 1], F32, name="warm_out")
         nc.vector.memset(warm[:], 0.0)
@@ -87,7 +87,7 @@ def tile_list_modp_ggelu_gateP_kernel(
 
         v_codes = []
         for g in range(J // PIECE):
-            codes = keep.tile([P, PIECE], U32, name=f"v_codes{g}", align_bytes=64)
+            codes = keep.tile([P, PIECE], U32, name="v_codes", tag=f"v_codes{g}", align_bytes=64)
             nc.vector.tensor_copy(codes[:], tab_codes[:].bitcast(U32).indirect(offsets[:, g * PIECE // 16 : (g + 1) * PIECE // 16]))
             v_codes.append(codes)
 
@@ -153,7 +153,7 @@ def tile_list_modp_ggelu_gateP_kernel(
             )
             if n == 0:
                 late_page("act0")
-        gws.append(weighted_gate(0, "act7"))
+        gws.append(weighted_gate(0, "gw0"))
         h_codes = keep.tile([P, J], U32, name="h_codes", align_bytes=64)
         h_sc = keep.tile([P, J], U8, name="h_sc", align_bytes=64)
         nc.vector.quantize_mx(h_codes[:].bitcast(FP8X4), h_sc[:], h_bf[:])
@@ -183,30 +183,35 @@ def tile_list_modp_ggelu_gateP_kernel(
                 nc.scalar.copy(y[:, h * HALF : (h + 1) * HALF], y_ps[:])
             ys.append(y)
 
+        out_bf = keep.tile([P, T, PACK], BF16, name="out_bf", align_bytes=64)
+        out_rows = out_0.rearrange("(p t) c -> t p c", t=PACK)
         edges = [0, 512, 1024, 1536, 1792, 2048]
         spans = [slice(lo, hi) for lo, hi in zip(edges, edges[1:])]
-        out_bf = [keep.tile([P, s.stop - s.start, PACK], BF16, name=f"out_bf{a}", align_bytes=64) for a, s in enumerate(spans)]
-        out_rows = out_0.rearrange("(p t) c -> t p c", t=PACK)
         for t in range(PACK):
             if t + 1 < PACK:
-                gws.append(weighted_gate(t + 1, ["act5", "act7", "act5"][t]))
+                gws.append(weighted_gate(t + 1, f"gw{t + 1}"))
             nc.vector.tensor_tensor(pages[t][:].indirect(offsets[:]), ys[t][:], gws[t][:], MULT)
             nc.sync.dma_start(out_rows[t], pages[t][:])
-            for a, s in enumerate(spans):
-                src = pages[t][:, s]
-                if a < 2 and t == PACK - 1:
-                    nc.vector.tensor_copy(out_bf[a][:, :, t], src)
-                elif a < 2 and t == PACK - 2:
-                    nc.scalar.copy(out_bf[a][:, :, t : t + 2], src.unsqueeze(2).to_broadcast([P, s.stop - s.start, 2]))
-                else:
-                    nc.scalar.copy(out_bf[a][:, :, t], src)
+            if t < PACK - 2:
+                nc.scalar.copy(out_bf[:, :, t], pages[t][:])
+            elif t == PACK - 2:
+                nc.scalar.copy(out_bf[:, : T // 2, t : t + 2], pages[t][:, : T // 2].unsqueeze(2).to_broadcast([P, T // 2, 2]))
+                nc.scalar.copy(out_bf[:, T // 2 :, t], pages[t][:, T // 2 :])
+            else:
+                for a, s in enumerate(spans):
+                    if a < 2:
+                        nc.vector.tensor_copy(out_bf[:, s, t], pages[t][:, s])
+                    else:
+                        nc.scalar.copy(out_bf[:, s, t], pages[t][:, s])
 
         out_sc = keep.tile([P, T], U8, name="out_sc", align_bytes=64)
+        out_codes = keep.tile([P, T], I32, name="out_codes", align_bytes=64)
         out_words = out_1[0].rearrange("p t i -> p (t i)").bitcast(I32)
+        stored = 0
         for a, s in enumerate(spans):
-            out_codes = keep.tile([P, s.stop - s.start], I32, name=f"out_codes{a}", align_bytes=64)
-            nc.vector.quantize_mx(out_codes[:].bitcast(FP8X4), out_sc[:, s], out_bf[a][:].rearrange("p c t -> p (c t)"))
-            nc.sync.dma_start(out_words[:, s], out_codes[:])
+            nc.vector.quantize_mx(out_codes[:, s].bitcast(FP8X4), out_sc[:, s], out_bf[:, s, :].rearrange("p c t -> p (c t)"))
+            if a in (1, 3, 4):
+                nc.sync.dma_start(out_words[:, stored : s.stop], out_codes[:, stored : s.stop])
+                stored = s.stop
         for q in range(4):
-            queue = nc.scalar if q % 2 == 0 else nc.sync
-            queue.dma_start(out_2[0, 4 * q : 4 * q + 4, :].bitcast(I32), out_sc[32 * q : 32 * q + 4, :].bitcast(I32))
+            nc.scalar.dma_start(out_2[0, 4 * q : 4 * q + 4, :].bitcast(I32), out_sc[32 * q : 32 * q + 4, :].bitcast(I32))

@@ -39,12 +39,8 @@ def tile_list_modp_ggelu_gateP_kernel(
         wg_plane = keep.tile([P, R], U8, name="wg_plane", tag="v_codes1", align_bytes=64)
         nc.vector.memset(tab_plane[:].bitcast(I32), 0)
         nc.vector.memset(wg_plane[:].bitcast(I32), 0)
-        warm = keep.tile([P, 1], F32, name="warm")
-        warm_out = keep.tile([P, 1], F32, name="warm_out")
-        nc.vector.memset(warm[:], 0.0)
-        nc.scalar.activation(warm_out[:], warm[:], GELU)
         pages = []
-        for t in range(2):
+        for t in range(PACK - 1):
             page = keep.tile([P, T], F32, name="page", tag=f"page{t}")
             nc.vector.memset(page[:].bitcast(I32), 0)
             pages.append(page)
@@ -58,7 +54,7 @@ def tile_list_modp_ggelu_gateP_kernel(
         nc.sync.dma_start(wg_raw[:], wg_words[0].bitcast(I32))
         wu_hi = keep.tile([P, PACK, R // 2], F32, name="wu_hi", align_bytes=64)
         nc.sync.dma_start(wu_hi[:], wu_rows[:, :, R // 2 :])
-        tab_codes = keep.tile([P, T], I32, name="tab_codes", tag="page2", align_bytes=64)
+        tab_codes = keep.tile([P, T], I32, name="tab_codes", align_bytes=64)
         nc.sync.dma_start(tab_codes[:], tab_words[0].rearrange("p t i -> p (t i)").bitcast(I32))
         for q in range(4):
             nc.sync.dma_start(wg_plane[32 * q : 32 * q + 4, :].bitcast(I32), wg_scales[0, 4 * q : 4 * q + 4, :].bitcast(I32))
@@ -137,7 +133,6 @@ def tile_list_modp_ggelu_gateP_kernel(
             nc.scalar.activation(act[:], ga[:].rearrange("p t j -> p j t"), GELU)
             return act
 
-        late_page("page2")
         gws = []
         h_bf = keep.tile([P, PACK * J], BF16, name="h_bf", align_bytes=64)
         acts = [gelu_chunk(0)]
@@ -151,8 +146,6 @@ def tile_list_modp_ggelu_gateP_kernel(
                 acts[n][:],
                 MULT,
             )
-            if n == 0:
-                late_page("act0")
         gws.append(weighted_gate(0, "gw0"))
         h_codes = keep.tile([P, J], U32, name="h_codes", align_bytes=64)
         h_sc = keep.tile([P, J], U8, name="h_sc", align_bytes=64)
@@ -192,6 +185,8 @@ def tile_list_modp_ggelu_gateP_kernel(
                 gws.append(weighted_gate(t + 1, f"gw{t + 1}"))
             nc.vector.tensor_tensor(pages[t][:].indirect(offsets[:]), ys[t][:], gws[t][:], MULT)
             nc.sync.dma_start(out_rows[t], pages[t][:])
+            if t == 0:
+                late_page("gw0")
             if t < PACK - 2:
                 nc.scalar.copy(out_bf[:, :, t], pages[t][:])
             elif t == PACK - 2:
@@ -214,4 +209,5 @@ def tile_list_modp_ggelu_gateP_kernel(
                 nc.sync.dma_start(out_words[:, stored : s.stop], out_codes[:, stored : s.stop])
                 stored = s.stop
         for q in range(4):
-            nc.scalar.dma_start(out_2[0, 4 * q : 4 * q + 4, :].bitcast(I32), out_sc[32 * q : 32 * q + 4, :].bitcast(I32))
+            queue = nc.scalar if q % 2 == 0 else nc.sync
+            queue.dma_start(out_2[0, 4 * q : 4 * q + 4, :].bitcast(I32), out_sc[32 * q : 32 * q + 4, :].bitcast(I32))

@@ -21,6 +21,10 @@ PACK = 4
 HALF = 512
 CHUNK = 128
 PIECE = 256
+STAGE_BANKS = 4
+WD_AFTER_CHUNK = 5
+SPAN_EDGES = [0, 512, 1024, 1536, 1792, 2048]
+VECTOR_SPANS = 2
 
 
 def tile_list_modp_ggelu_gateP_kernel(
@@ -101,15 +105,10 @@ def tile_list_modp_ggelu_gateP_kernel(
             nc.sync.dma_start(gate[:], gT_rows[t])
             gates.append(gate)
 
-        def weighted_gate(t, tag):
-            gw = keep.tile([P, J], F32, name="gw", tag=tag, align_bytes=64)
+        def weighted_gate(t):
+            gw = keep.tile([P, J], F32, name="gw", tag=f"gw{t}", align_bytes=64)
             nc.vector.tensor_tensor(gw[:], gates[t][:].indirect(offsets[:]), wgo_sb[:], MULT)
             return gw
-
-        def late_page(tag):
-            page = keep.tile([P, T], F32, name="page", tag=tag, align_bytes=64)
-            nc.gpsimd.memset(page[:], 0.0)
-            pages.append(page)
 
         def product(n, bank, w_codes, w_dtype, width, w_sc):
             acc = psum.tile([P, PACK, CHUNK], F32, name="acc", tag=bank)
@@ -128,7 +127,7 @@ def tile_list_modp_ggelu_gateP_kernel(
             return acc
 
         def gelu_chunk(n):
-            ga = product(n, f"ga{n % 4}", wg_codes, FP4X4, 2 * P, wg_sc)
+            ga = product(n, f"ga{n % STAGE_BANKS}", wg_codes, FP4X4, 2 * P, wg_sc)
             act = keep.tile([P, CHUNK, PACK], F32, name="act", tag=f"act{n}", align_bytes=64)
             nc.scalar.activation(act[:], ga[:].rearrange("p t j -> p j t"), GELU)
             return act
@@ -139,27 +138,28 @@ def tile_list_modp_ggelu_gateP_kernel(
         for n in range(J // CHUNK):
             if n + 1 < J // CHUNK:
                 acts.append(gelu_chunk(n + 1))
-            ub = product(n, f"ub{n % 4}", wu_codes, FP8X4, P, wu_sc)
+            ub = product(n, f"ub{n % STAGE_BANKS}", wu_codes, FP8X4, P, wu_sc)
             nc.vector.tensor_tensor(
                 h_bf[:, PACK * n * CHUNK : PACK * (n + 1) * CHUNK].rearrange("p (j t) -> p j t", t=PACK),
                 ub[:].rearrange("p t j -> p j t"),
                 acts[n][:],
                 MULT,
             )
-        gws.append(weighted_gate(0, "gw0"))
+        gws.append(weighted_gate(0))
         h_codes = keep.tile([P, J], U32, name="h_codes", align_bytes=64)
         h_sc = keep.tile([P, J], U8, name="h_sc", align_bytes=64)
         nc.vector.quantize_mx(h_codes[:].bitcast(FP8X4), h_sc[:], h_bf[:])
 
         wd_codes = keep.tile([P, N], U32, name="wd_codes", align_bytes=64)
-        wd_bf = keep.tile([P, PACK * N], BF16, name="wd_bf", tag="act5", align_bytes=64)
+        wd_bf = keep.tile([P, PACK * N], BF16, name="wd_bf", tag=f"act{WD_AFTER_CHUNK}", align_bytes=64)
         nc.scalar.copy(
             wd_bf[:].rearrange("p (t m s) -> p m s t", t=PACK, s=PACK),
             wd_raw[:].rearrange("p s (m t) -> p m s t", t=PACK),
         )
         nc.vector.quantize_mx(wd_codes[:].bitcast(FP8X4), wd_sc[:], wd_bf[:])
+
         ys = []
-        y_banks = ["ga0", "ga1", "ga2", "ga3", "ub0", "ub1", "ub2", "ub3"]
+        y_banks = [f"{kind}{b}" for kind in ("ga", "ub") for b in range(STAGE_BANKS)]
         for t in range(PACK):
             y = keep.tile([P, J], F32, name=f"y{t}")
             for h in range(halves):
@@ -178,23 +178,25 @@ def tile_list_modp_ggelu_gateP_kernel(
 
         out_bf = keep.tile([P, T, PACK], BF16, name="out_bf", align_bytes=64)
         out_rows = out_0.rearrange("(p t) c -> t p c", t=PACK)
-        edges = [0, 512, 1024, 1536, 1792, 2048]
-        spans = [slice(lo, hi) for lo, hi in zip(edges, edges[1:])]
+        spans = [slice(lo, hi) for lo, hi in zip(SPAN_EDGES, SPAN_EDGES[1:])]
+        shared = SPAN_EDGES[VECTOR_SPANS]
         for t in range(PACK):
             if t + 1 < PACK:
-                gws.append(weighted_gate(t + 1, f"gw{t + 1}"))
+                gws.append(weighted_gate(t + 1))
             nc.vector.tensor_tensor(pages[t][:].indirect(offsets[:]), ys[t][:], gws[t][:], MULT)
             nc.sync.dma_start(out_rows[t], pages[t][:])
             if t == 0:
-                late_page("gw0")
+                page = keep.tile([P, T], F32, name="page", tag="gw0", align_bytes=64)
+                nc.gpsimd.memset(page[:], 0.0)
+                pages.append(page)
             if t < PACK - 2:
                 nc.scalar.copy(out_bf[:, :, t], pages[t][:])
             elif t == PACK - 2:
-                nc.scalar.copy(out_bf[:, : T // 2, t : t + 2], pages[t][:, : T // 2].unsqueeze(2).to_broadcast([P, T // 2, 2]))
-                nc.scalar.copy(out_bf[:, T // 2 :, t], pages[t][:, T // 2 :])
+                nc.scalar.copy(out_bf[:, :shared, t : t + 2], pages[t][:, :shared].unsqueeze(2).to_broadcast([P, shared, 2]))
+                nc.scalar.copy(out_bf[:, shared:, t], pages[t][:, shared:])
             else:
                 for a, s in enumerate(spans):
-                    if a < 2:
+                    if a < VECTOR_SPANS:
                         nc.vector.tensor_copy(out_bf[:, s, t], pages[t][:, s])
                     else:
                         nc.scalar.copy(out_bf[:, s, t], pages[t][:, s])
@@ -202,12 +204,9 @@ def tile_list_modp_ggelu_gateP_kernel(
         out_sc = keep.tile([P, T], U8, name="out_sc", align_bytes=64)
         out_codes = keep.tile([P, T], I32, name="out_codes", align_bytes=64)
         out_words = out_1[0].rearrange("p t i -> p (t i)").bitcast(I32)
-        stored = 0
-        for a, s in enumerate(spans):
+        for s in spans:
             nc.vector.quantize_mx(out_codes[:, s].bitcast(FP8X4), out_sc[:, s], out_bf[:, s, :].rearrange("p c t -> p (c t)"))
-            if a in (1, 3, 4):
-                nc.sync.dma_start(out_words[:, stored : s.stop], out_codes[:, stored : s.stop])
-                stored = s.stop
+            nc.sync.dma_start(out_words[:, s], out_codes[:, s])
         for q in range(4):
             queue = nc.scalar if q % 2 == 0 else nc.sync
             queue.dma_start(out_2[0, 4 * q : 4 * q + 4, :].bitcast(I32), out_sc[32 * q : 32 * q + 4, :].bitcast(I32))

@@ -1,6 +1,7 @@
 from contextlib import ExitStack
 
 import concourse.mybir as mybir
+from concourse.masks import make_identity
 
 K, R, N, T, J = 512, 512, 512, 2048, 1024
 FLOPS = 2 * J * (2 * K * R + R * N)
@@ -14,6 +15,7 @@ U8 = mybir.dt.uint8
 FP8X4 = mybir.dt.float8_e4m3fn_x4
 FP4X4 = mybir.dt.float4_e2m1fn_x4
 MULT = mybir.AluOpType.mult
+COPY = mybir.ActivationFunctionType.Copy
 GELU = mybir.ActivationFunctionType.Gelu_apprx_tanh
 
 P = 128
@@ -21,8 +23,9 @@ PACK = 4
 HALF = 512
 CHUNK = 128
 PIECE = 256
+PAGES = 2
 STAGE_BANKS = 4
-WD_AFTER_CHUNK = 5
+H_EDGES = [0, 4, 6, 8]
 SPAN_EDGES = [0, 512, 1024, 1536, 1792, 2048]
 VECTOR_SPANS = 2
 
@@ -40,11 +43,11 @@ def tile_list_modp_ggelu_gateP_kernel(
         nc.sync.dma_start(offsets[:], offs)
 
         tab_plane = keep.tile([P, T], U8, name="tab_plane", align_bytes=64)
-        wg_plane = keep.tile([P, R], U8, name="wg_plane", tag="v_codes1", align_bytes=64)
+        wg_plane = keep.tile([P, R], U8, name="wg_plane", align_bytes=64)
         nc.vector.memset(tab_plane[:].bitcast(I32), 0)
         nc.vector.memset(wg_plane[:].bitcast(I32), 0)
         pages = []
-        for t in range(PACK - 1):
+        for t in range(PAGES):
             page = keep.tile([P, T], F32, name="page", tag=f"page{t}")
             nc.vector.memset(page[:].bitcast(I32), 0)
             pages.append(page)
@@ -58,10 +61,10 @@ def tile_list_modp_ggelu_gateP_kernel(
         nc.sync.dma_start(wg_raw[:], wg_words[0].bitcast(I32))
         wu_hi = keep.tile([P, PACK, R // 2], F32, name="wu_hi", align_bytes=64)
         nc.sync.dma_start(wu_hi[:], wu_rows[:, :, R // 2 :])
-        tab_codes = keep.tile([P, T], I32, name="tab_codes", align_bytes=64)
-        nc.sync.dma_start(tab_codes[:], tab_words[0].rearrange("p t i -> p (t i)").bitcast(I32))
         for q in range(4):
             nc.sync.dma_start(wg_plane[32 * q : 32 * q + 4, :].bitcast(I32), wg_scales[0, 4 * q : 4 * q + 4, :].bitcast(I32))
+        tab_codes = keep.tile([P, T], I32, name="tab_codes", align_bytes=64)
+        nc.sync.dma_start(tab_codes[:], tab_words[0].rearrange("p t i -> p (t i)").bitcast(I32))
 
         v_sc = keep.tile([P, J], U8, name="v_sc", align_bytes=64)
         nc.vector.tensor_copy(v_sc[:], tab_plane[:].indirect(offsets[:]))
@@ -91,23 +94,29 @@ def tile_list_modp_ggelu_gateP_kernel(
             nc.vector.tensor_copy(codes[:], tab_codes[:].bitcast(U32).indirect(offsets[:, g * PIECE // 16 : (g + 1) * PIECE // 16]))
             v_codes.append(codes)
 
-        wd_raw = keep.tile([P, PACK, N], F32, name="wd_raw", align_bytes=64)
-        nc.sync.dma_start(wd_raw[:], wd.rearrange("(p s) n -> p s n", s=PACK))
-        wgo_sb = keep.tile([P, J], F32, name="wgo_sb", tag="wgo", align_bytes=64)
-        nc.sync.dma_start(wgo_sb[:], wgo)
-
-        wd_sc = keep.tile([P, N], U8, name="wd_sc", align_bytes=64)
-
         gT_rows = gT.rearrange("(p t) c -> t p c", t=PACK)
-        gates = []
-        for t in range(PACK):
-            gate = keep.tile([P, T], F32, name="gate", tag=f"gate{t}", align_bytes=64)
-            nc.sync.dma_start(gate[:], gT_rows[t])
-            gates.append(gate)
+        gates = [keep.tile([P, T], F32, name="gate", tag=f"gate{t}", align_bytes=64) for t in range(PACK)]
+        wd_raw = keep.tile([P, PACK, N], F32, name="wd_raw", align_bytes=64)
+        wgo_sb = keep.tile([P, J], F32, name="wgo_sb", tag="wgo", align_bytes=64)
+        wgo_col = keep.tile([P, J // P], F32, name="wgo_col", align_bytes=64)
+        nc.sync.dma_start(gates[1][:], gT_rows[1])
+        nc.sync.dma_start(gates[2][:], gT_rows[2])
+        nc.sync.dma_start(gates[3][:], gT_rows[3])
+        nc.sync.dma_start(wd_raw[:], wd.rearrange("(p s) n -> p s n", s=PACK))
+        nc.sync.dma_start(wgo_sb[:], wgo)
+        nc.sync.dma_start(gates[0][:], gT_rows[0])
+        with nc.allow_non_contiguous_dma(reason="one weight for each partition and block of tokens"):
+            nc.sync.dma_start(wgo_col[:], wgo[0].rearrange("(b p) -> p b", p=P))
+        wd_sc = keep.tile([P, N], U8, name="wd_sc", align_bytes=64)
+        ident = keep.tile([P, P], F32, name="ident", align_bytes=64)
+        make_identity(nc, ident[:])
 
-        def weighted_gate(t):
+        def picked_gate(t):
             gw = keep.tile([P, J], F32, name="gw", tag=f"gw{t}", align_bytes=64)
-            nc.vector.tensor_tensor(gw[:], gates[t][:].indirect(offsets[:]), wgo_sb[:], MULT)
+            if t == 0:
+                nc.vector.tensor_tensor(gw[:], gates[t][:].indirect(offsets[:]), wgo_sb[:], MULT)
+            else:
+                nc.vector.tensor_copy(gw[:], gates[t][:].indirect(offsets[:]))
             return gw
 
         def product(n, bank, w_codes, w_dtype, width, w_sc):
@@ -132,74 +141,99 @@ def tile_list_modp_ggelu_gateP_kernel(
             nc.scalar.activation(act[:], ga[:].rearrange("p t j -> p j t"), GELU)
             return act
 
-        gws = []
-        h_bf = keep.tile([P, PACK * J], BF16, name="h_bf", align_bytes=64)
-        acts = [gelu_chunk(0)]
-        for n in range(J // CHUNK):
-            if n + 1 < J // CHUNK:
-                acts.append(gelu_chunk(n + 1))
-            ub = product(n, f"ub{n % STAGE_BANKS}", wu_codes, FP8X4, P, wu_sc)
-            nc.vector.tensor_tensor(
-                h_bf[:, PACK * n * CHUNK : PACK * (n + 1) * CHUNK].rearrange("p (j t) -> p j t", t=PACK),
-                ub[:].rearrange("p t j -> p j t"),
-                acts[n][:],
-                MULT,
-            )
-        gws.append(weighted_gate(0))
+        gws = {t: picked_gate(t) for t in range(1, PACK)}
         h_codes = keep.tile([P, J], U32, name="h_codes", align_bytes=64)
         h_sc = keep.tile([P, J], U8, name="h_sc", align_bytes=64)
-        nc.vector.quantize_mx(h_codes[:].bitcast(FP8X4), h_sc[:], h_bf[:])
+        h_parts = []
+        for lo, hi in zip(H_EDGES, H_EDGES[1:]):
+            h_bf = keep.tile([P, (hi - lo) * CHUNK, PACK], BF16, name="h_bf", tag=f"h_bf{lo}", align_bytes=64)
+            h_parts.append(h_bf)
+            for n in range(lo, hi):
+                act = gelu_chunk(n)
+                ub = product(n, f"ub{n % STAGE_BANKS}", wu_codes, FP8X4, P, wu_sc)
+                h_chunk = h_bf[:, (n - lo) * CHUNK : (n - lo + 1) * CHUNK, :]
+                if lo == H_EDGES[-2]:
+                    nc.vector.tensor_tensor(h_chunk, ub[:].rearrange("p t j -> p j t"), act[:], MULT)
+                else:
+                    ub_sb = keep.tile([P, CHUNK, PACK], F32, name="ub_sb", tag=f"ub_sb{n}", align_bytes=64)
+                    nc.scalar.copy(ub_sb[:], ub[:].rearrange("p t j -> p j t"))
+                    nc.gpsimd.tensor_tensor(h_chunk, ub_sb[:], act[:], MULT)
+        for lo, hi, h_bf in zip(H_EDGES, H_EDGES[1:], h_parts):
+            cols = slice(lo * CHUNK, hi * CHUNK)
+            nc.vector.quantize_mx(h_codes[:, cols].bitcast(FP8X4), h_sc[:, cols], h_bf[:].rearrange("p j t -> p (j t)"))
 
         wd_codes = keep.tile([P, N], U32, name="wd_codes", align_bytes=64)
-        wd_bf = keep.tile([P, PACK * N], BF16, name="wd_bf", tag=f"act{WD_AFTER_CHUNK}", align_bytes=64)
+        wd_bf = keep.tile([P, PACK * N], BF16, name="wd_bf", tag=f"v_codes{J // PIECE - 1}", align_bytes=64)
         nc.scalar.copy(
             wd_bf[:].rearrange("p (t m s) -> p m s t", t=PACK, s=PACK),
             wd_raw[:].rearrange("p s (m t) -> p m s t", t=PACK),
         )
         nc.vector.quantize_mx(wd_codes[:].bitcast(FP8X4), wd_sc[:], wd_bf[:])
 
-        ys = []
-        y_banks = [f"{kind}{b}" for kind in ("ga", "ub") for b in range(STAGE_BANKS)]
-        for t in range(PACK):
-            y = keep.tile([P, J], F32, name=f"y{t}")
-            for h in range(halves):
-                y_ps = psum.tile([P, HALF], F32, name="y_ps", tag=y_banks[t * halves + h])
-                nc.tensor.matmul_mx(
-                    y_ps[:],
-                    lhsT=wd_codes[:, P * t : P * (t + 1)].bitcast(FP8X4),
-                    lhsT_scale=wd_sc[:, P * t : P * (t + 1)],
-                    rhs=h_codes[:, h * HALF : (h + 1) * HALF].bitcast(FP8X4),
-                    rhs_scale=h_sc[:, h * HALF : (h + 1) * HALF],
-                    start=True,
-                    stop=True,
-                )
-                nc.scalar.copy(y[:, h * HALF : (h + 1) * HALF], y_ps[:])
-            ys.append(y)
+        gws[0] = picked_gate(0)
 
-        out_bf = keep.tile([P, T, PACK], BF16, name="out_bf", align_bytes=64)
+        banks = [f"{kind}{b}" for kind in ("ga", "ub") for b in range(STAGE_BANKS)]
+        ys = [keep.tile([P, J], F32, name=f"y{t}") for t in range(PACK)]
+        for h in range(halves):
+            y_ps = psum.tile([P, HALF], F32, name="y_ps", tag=banks[h])
+            nc.tensor.matmul_mx(
+                y_ps[:],
+                lhsT=wd_codes[:, :P].bitcast(FP8X4),
+                lhsT_scale=wd_sc[:, :P],
+                rhs=h_codes[:, h * HALF : (h + 1) * HALF].bitcast(FP8X4),
+                rhs_scale=h_sc[:, h * HALF : (h + 1) * HALF],
+                start=True,
+                stop=True,
+            )
+            nc.scalar.copy(ys[0][:, h * HALF : (h + 1) * HALF], y_ps[:])
+        per_bank = HALF // P
+        for t in range(1, PACK):
+            y_tok = keep.tile([P, J // P, P], F32, name="y_tok", tag=f"y_tok{t}", align_bytes=64)
+            for h in range(halves):
+                tok_ps = psum.tile([P, per_bank, P], F32, name="tok_ps", tag=banks[(4 * t - 2 + h) % len(banks)])
+                for i in range(per_bank):
+                    b = h * per_bank + i
+                    nc.tensor.matmul_mx(
+                        tok_ps[:, i, :],
+                        lhsT=h_codes[:, P * b : P * (b + 1)].bitcast(FP8X4),
+                        lhsT_scale=h_sc[:, P * b : P * (b + 1)],
+                        rhs=wd_codes[:, P * t : P * (t + 1)].bitcast(FP8X4),
+                        rhs_scale=wd_sc[:, P * t : P * (t + 1)],
+                        start=True,
+                        stop=True,
+                    )
+                for i in range(per_bank):
+                    b = h * per_bank + i
+                    nc.scalar.activation(y_tok[:, b, :], tok_ps[:, i, :], COPY, scale=wgo_col[:, b : b + 1])
+            for h in range(halves):
+                back_ps = psum.tile([P, per_bank, P], F32, name="back_ps", tag=banks[(4 * t + h) % len(banks)])
+                for i in range(per_bank):
+                    nc.tensor.transpose(back_ps[:, i, :], y_tok[:, h * per_bank + i, :], ident[:])
+                nc.scalar.copy(ys[t][:, h * HALF : (h + 1) * HALF], back_ps[:].rearrange("p i j -> p (i j)"))
+
+        out_bf = keep.tile([P, T, PACK], BF16, name="out_bf", tag=f"y_tok{PACK - 1}", align_bytes=64)
         out_rows = out_0.rearrange("(p t) c -> t p c", t=PACK)
         spans = [slice(lo, hi) for lo, hi in zip(SPAN_EDGES, SPAN_EDGES[1:])]
         shared = SPAN_EDGES[VECTOR_SPANS]
         for t in range(PACK):
-            if t + 1 < PACK:
-                gws.append(weighted_gate(t + 1))
-            nc.vector.tensor_tensor(pages[t][:].indirect(offsets[:]), ys[t][:], gws[t][:], MULT)
-            nc.sync.dma_start(out_rows[t], pages[t][:])
-            if t == 0:
-                page = keep.tile([P, T], F32, name="page", tag="gw0", align_bytes=64)
-                nc.gpsimd.memset(page[:], 0.0)
-                pages.append(page)
+            if t == PAGES:
+                third = keep.tile([P, T], F32, name="third", tag="gate0", align_bytes=64)
+                nc.gpsimd.memset(third[:], 0.0)
+                pages.append(third)
+            page = pages[t % (PAGES + 1)]
+            nc.vector.tensor_tensor(page[:].indirect(offsets[:]), ys[t][:], gws[t][:], MULT)
+            nc.sync.dma_start(out_rows[t], page[:])
             if t < PACK - 2:
-                nc.scalar.copy(out_bf[:, :, t], pages[t][:])
+                nc.scalar.copy(out_bf[:, :, t], page[:])
             elif t == PACK - 2:
-                nc.scalar.copy(out_bf[:, :shared, t : t + 2], pages[t][:, :shared].unsqueeze(2).to_broadcast([P, shared, 2]))
-                nc.scalar.copy(out_bf[:, shared:, t], pages[t][:, shared:])
+                nc.scalar.copy(out_bf[:, :shared, t : t + 2], page[:, :shared].unsqueeze(2).to_broadcast([P, shared, 2]))
+                nc.scalar.copy(out_bf[:, shared:, t], page[:, shared:])
             else:
                 for a, s in enumerate(spans):
                     if a < VECTOR_SPANS:
-                        nc.vector.tensor_copy(out_bf[:, s, t], pages[t][:, s])
+                        nc.vector.tensor_copy(out_bf[:, s, t], page[:, s])
                     else:
-                        nc.scalar.copy(out_bf[:, s, t], pages[t][:, s])
+                        nc.scalar.copy(out_bf[:, s, t], page[:, s])
 
         out_sc = keep.tile([P, T], U8, name="out_sc", align_bytes=64)
         out_codes = keep.tile([P, T], I32, name="out_codes", align_bytes=64)

@@ -25,7 +25,8 @@ CHUNK = 128
 PIECE = 256
 PAGES = 2
 STAGE_BANKS = 4
-H_EDGES = [0, 4, 6, 8]
+H_EDGES = [0, 4, 8]
+STRAIGHT = 2
 SPAN_EDGES = [0, 512, 1024, 1536, 1792, 2048]
 VECTOR_SPANS = 2
 
@@ -98,22 +99,19 @@ def tile_list_modp_ggelu_gateP_kernel(
         gates = [keep.tile([P, T], F32, name="gate", tag=f"gate{t}", align_bytes=64) for t in range(PACK)]
         wd_raw = keep.tile([P, PACK, N], F32, name="wd_raw", align_bytes=64)
         wgo_sb = keep.tile([P, J], F32, name="wgo_sb", tag="wgo", align_bytes=64)
-        wgo_col = keep.tile([P, J // P], F32, name="wgo_col", align_bytes=64)
-        nc.sync.dma_start(gates[1][:], gT_rows[1])
-        nc.sync.dma_start(gates[2][:], gT_rows[2])
-        nc.sync.dma_start(gates[3][:], gT_rows[3])
+        for t in range(STRAIGHT, PACK):
+            nc.sync.dma_start(gates[t][:], gT_rows[t])
         nc.sync.dma_start(wd_raw[:], wd.rearrange("(p s) n -> p s n", s=PACK))
         nc.sync.dma_start(wgo_sb[:], wgo)
-        nc.sync.dma_start(gates[0][:], gT_rows[0])
-        with nc.allow_non_contiguous_dma(reason="one weight for each partition and block of tokens"):
-            nc.sync.dma_start(wgo_col[:], wgo[0].rearrange("(b p) -> p b", p=P))
+        for t in range(STRAIGHT):
+            nc.sync.dma_start(gates[t][:], gT_rows[t])
         wd_sc = keep.tile([P, N], U8, name="wd_sc", align_bytes=64)
         ident = keep.tile([P, P], F32, name="ident", align_bytes=64)
         make_identity(nc, ident[:])
 
         def picked_gate(t):
             gw = keep.tile([P, J], F32, name="gw", tag=f"gw{t}", align_bytes=64)
-            if t == 0:
+            if t < STRAIGHT:
                 nc.vector.tensor_tensor(gw[:], gates[t][:].indirect(offsets[:]), wgo_sb[:], MULT)
             else:
                 nc.vector.tensor_copy(gw[:], gates[t][:].indirect(offsets[:]))
@@ -141,7 +139,7 @@ def tile_list_modp_ggelu_gateP_kernel(
             nc.scalar.activation(act[:], ga[:].rearrange("p t j -> p j t"), GELU)
             return act
 
-        gws = {t: picked_gate(t) for t in range(1, PACK)}
+        gws = {t: picked_gate(t) for t in range(STRAIGHT, PACK)}
         h_codes = keep.tile([P, J], U32, name="h_codes", align_bytes=64)
         h_sc = keep.tile([P, J], U8, name="h_sc", align_bytes=64)
         h_parts = []
@@ -173,49 +171,62 @@ def tile_list_modp_ggelu_gateP_kernel(
         gws[0] = picked_gate(0)
 
         banks = [f"{kind}{b}" for kind in ("ga", "ub") for b in range(STAGE_BANKS)]
-        ys = [keep.tile([P, J], F32, name=f"y{t}") for t in range(PACK)]
-        for h in range(halves):
-            y_ps = psum.tile([P, HALF], F32, name="y_ps", tag=banks[h])
-            nc.tensor.matmul_mx(
-                y_ps[:],
-                lhsT=wd_codes[:, :P].bitcast(FP8X4),
-                lhsT_scale=wd_sc[:, :P],
-                rhs=h_codes[:, h * HALF : (h + 1) * HALF].bitcast(FP8X4),
-                rhs_scale=h_sc[:, h * HALF : (h + 1) * HALF],
-                start=True,
-                stop=True,
-            )
-            nc.scalar.copy(ys[0][:, h * HALF : (h + 1) * HALF], y_ps[:])
         per_bank = HALF // P
-        for t in range(1, PACK):
-            y_tok = keep.tile([P, J // P, P], F32, name="y_tok", tag=f"y_tok{t}", align_bytes=64)
+        wgo_col = keep.tile([P, J // P], F32, name="wgo_col", align_bytes=64)
+        for h in range(halves):
+            col_ps = psum.tile([P, per_bank, P], F32, name="col_ps", tag=banks[h])
+            for i in range(per_bank):
+                b = h * per_bank + i
+                nc.tensor.transpose(col_ps[:, i, :], wgo_sb[:, P * b : P * (b + 1)], ident[:])
+            nc.scalar.copy(wgo_col[:, h * per_bank : (h + 1) * per_bank], col_ps[:, :, 0])
+
+        ys = [keep.tile([P, J], F32, name=f"y{t}") for t in range(PACK)]
+        for t in range(STRAIGHT):
             for h in range(halves):
-                tok_ps = psum.tile([P, per_bank, P], F32, name="tok_ps", tag=banks[(4 * t - 2 + h) % len(banks)])
-                for i in range(per_bank):
-                    b = h * per_bank + i
-                    nc.tensor.matmul_mx(
-                        tok_ps[:, i, :],
-                        lhsT=h_codes[:, P * b : P * (b + 1)].bitcast(FP8X4),
-                        lhsT_scale=h_sc[:, P * b : P * (b + 1)],
-                        rhs=wd_codes[:, P * t : P * (t + 1)].bitcast(FP8X4),
-                        rhs_scale=wd_sc[:, P * t : P * (t + 1)],
-                        start=True,
-                        stop=True,
-                    )
-                for i in range(per_bank):
-                    b = h * per_bank + i
-                    nc.scalar.activation(y_tok[:, b, :], tok_ps[:, i, :], COPY, scale=wgo_col[:, b : b + 1])
+                y_ps = psum.tile([P, HALF], F32, name="y_ps", tag=banks[2 + halves * t + h])
+                nc.tensor.matmul_mx(
+                    y_ps[:],
+                    lhsT=wd_codes[:, P * t : P * (t + 1)].bitcast(FP8X4),
+                    lhsT_scale=wd_sc[:, P * t : P * (t + 1)],
+                    rhs=h_codes[:, h * HALF : (h + 1) * HALF].bitcast(FP8X4),
+                    rhs_scale=h_sc[:, h * HALF : (h + 1) * HALF],
+                    start=True,
+                    stop=True,
+                )
+                nc.scalar.copy(ys[t][:, h * HALF : (h + 1) * HALF], y_ps[:])
+        turned = PACK - STRAIGHT
+        y_tok = keep.tile([P, J // P, turned * P], F32, name="y_tok", tag="y_tok", align_bytes=64)
+        pair = HALF // (turned * P)
+        for g in range(J // P // pair):
+            tok_ps = psum.tile([P, pair, turned * P], F32, name="tok_ps", tag=banks[(6 + g) % len(banks)])
+            for i in range(pair):
+                b = g * pair + i
+                nc.tensor.matmul_mx(
+                    tok_ps[:, i, :],
+                    lhsT=h_codes[:, P * b : P * (b + 1)].bitcast(FP8X4),
+                    lhsT_scale=h_sc[:, P * b : P * (b + 1)],
+                    rhs=wd_codes[:, P * STRAIGHT :].bitcast(FP8X4),
+                    rhs_scale=wd_sc[:, P * STRAIGHT :],
+                    start=True,
+                    stop=True,
+                )
+            for i in range(pair):
+                b = g * pair + i
+                nc.scalar.activation(y_tok[:, b, :], tok_ps[:, i, :], COPY, scale=wgo_col[:, b : b + 1])
+        for t in range(STRAIGHT, PACK):
             for h in range(halves):
-                back_ps = psum.tile([P, per_bank, P], F32, name="back_ps", tag=banks[(4 * t + h) % len(banks)])
+                back_ps = psum.tile([P, per_bank, P], F32, name="back_ps", tag=banks[2 + halves * (t - STRAIGHT) + h])
                 for i in range(per_bank):
-                    nc.tensor.transpose(back_ps[:, i, :], y_tok[:, h * per_bank + i, :], ident[:])
+                    nc.tensor.transpose(back_ps[:, i, :], y_tok[:, h * per_bank + i, P * (t - STRAIGHT) : P * (t - STRAIGHT + 1)], ident[:])
                 nc.scalar.copy(ys[t][:, h * HALF : (h + 1) * HALF], back_ps[:].rearrange("p i j -> p (i j)"))
 
-        out_bf = keep.tile([P, T, PACK], BF16, name="out_bf", tag=f"y_tok{PACK - 1}", align_bytes=64)
+        out_bf = keep.tile([P, T, PACK], BF16, name="out_bf", tag="y_tok", align_bytes=64)
         out_rows = out_0.rearrange("(p t) c -> t p c", t=PACK)
         spans = [slice(lo, hi) for lo, hi in zip(SPAN_EDGES, SPAN_EDGES[1:])]
         shared = SPAN_EDGES[VECTOR_SPANS]
         for t in range(PACK):
+            if 0 < t < STRAIGHT:
+                gws[t] = picked_gate(t)
             if t == PAGES:
                 third = keep.tile([P, T], F32, name="third", tag="gate0", align_bytes=64)
                 nc.gpsimd.memset(third[:], 0.0)

@@ -22,10 +22,11 @@ P = 128
 PACK = 4
 HALF = 512
 CHUNK = 128
-PIECE = 256
-PAGES = 2
+WORD_EDGES = [0, 256, 1024]
+PAGES = 3
 STAGE_BANKS = 4
-H_EDGES = [0, 4, 8]
+H_EDGES = [0, 1, 2, 3, 4, 8]
+GPSIMD_CHUNKS = 3
 STRAIGHT = 2
 SPAN_EDGES = [0, 512, 1024, 1536, 1792, 2048]
 VECTOR_SPANS = 2
@@ -44,28 +45,26 @@ def tile_list_modp_ggelu_gateP_kernel(
         nc.sync.dma_start(offsets[:], offs)
 
         tab_plane = keep.tile([P, T], U8, name="tab_plane", align_bytes=64)
-        wg_plane = keep.tile([P, R], U8, name="wg_plane", align_bytes=64)
+        wg_plane = keep.tile([P, R], U8, name="wg_plane", tag="v_codes1", align_bytes=64)
         nc.vector.memset(tab_plane[:].bitcast(I32), 0)
         nc.vector.memset(wg_plane[:].bitcast(I32), 0)
-        pages = []
-        for t in range(PAGES):
-            page = keep.tile([P, T], F32, name="page", tag=f"page{t}")
-            nc.vector.memset(page[:].bitcast(I32), 0)
-            pages.append(page)
+        first_page = keep.tile([P, T], F32, name="first_page")
+        nc.vector.memset(first_page[:].bitcast(I32), 0)
+        pages = [first_page]
 
-        wu_rows = wu.rearrange("(p j) c -> p j c", j=PACK)
-        wu_lo = keep.tile([P, PACK, R // 2], F32, name="wu_lo", align_bytes=64)
-        nc.sync.dma_start(wu_lo[:], wu_rows[:, :, : R // 2])
-        for q in range(4):
-            nc.sync.dma_start(tab_plane[32 * q : 32 * q + 4, :].bitcast(I32), tab_scales[0, 4 * q : 4 * q + 4, :].bitcast(I32))
         wg_raw = keep.tile([P, R // 2], I32, name="wg_raw", align_bytes=64)
         nc.sync.dma_start(wg_raw[:], wg_words[0].bitcast(I32))
-        wu_hi = keep.tile([P, PACK, R // 2], F32, name="wu_hi", align_bytes=64)
-        nc.sync.dma_start(wu_hi[:], wu_rows[:, :, R // 2 :])
         for q in range(4):
-            nc.sync.dma_start(wg_plane[32 * q : 32 * q + 4, :].bitcast(I32), wg_scales[0, 4 * q : 4 * q + 4, :].bitcast(I32))
+            nc.sync.dma_start(tab_plane[32 * q : 32 * q + 4, :].bitcast(I32), tab_scales[0, 4 * q : 4 * q + 4, :].bitcast(I32))
         tab_codes = keep.tile([P, T], I32, name="tab_codes", align_bytes=64)
         nc.sync.dma_start(tab_codes[:], tab_words[0].rearrange("p t i -> p (t i)").bitcast(I32))
+        for q in range(4):
+            nc.sync.dma_start(wg_plane[32 * q : 32 * q + 4, :].bitcast(I32), wg_scales[0, 4 * q : 4 * q + 4, :].bitcast(I32))
+        wu_rows = wu.rearrange("(p j) c -> p j c", j=PACK)
+        wu_lo = keep.tile([P, PACK, R // 2], F32, name="wu_lo", tag="act1", align_bytes=64)
+        nc.sync.dma_start(wu_lo[:], wu_rows[:, :, : R // 2])
+        wu_hi = keep.tile([P, PACK, R // 2], F32, name="wu_hi", align_bytes=64)
+        nc.sync.dma_start(wu_hi[:], wu_rows[:, :, R // 2 :])
 
         v_sc = keep.tile([P, J], U8, name="v_sc", align_bytes=64)
         nc.vector.tensor_copy(v_sc[:], tab_plane[:].indirect(offsets[:]))
@@ -81,19 +80,19 @@ def tile_list_modp_ggelu_gateP_kernel(
             wg_plane[:].rearrange("p (m t) -> p t m", t=PACK),
         )
 
+        v_codes = []
+        for g, (lo, hi) in enumerate(zip(WORD_EDGES, WORD_EDGES[1:])):
+            codes = keep.tile([P, hi - lo], U32, name="v_codes", tag=f"v_codes{g}", align_bytes=64)
+            nc.vector.tensor_copy(codes[:], tab_codes[:].bitcast(U32).indirect(offsets[:, lo // 16 : hi // 16]))
+            v_codes.append(codes)
+
         wu_bf = keep.tile([P, PACK * R], BF16, name="wu_bf", align_bytes=64)
         wu_dealt = wu_bf[:].rearrange("p (t m j) -> p m j t", t=PACK, j=PACK)
         nc.scalar.copy(wu_dealt[:, : P // 2], wu_lo[:].rearrange("p j (m t) -> p m j t", t=PACK))
-        nc.scalar.copy(wu_dealt[:, P // 2 :], wu_hi[:].rearrange("p j (m t) -> p m j t", t=PACK))
+        nc.vector.tensor_copy(wu_dealt[:, P // 2 :], wu_hi[:].rearrange("p j (m t) -> p m j t", t=PACK))
         wu_codes = keep.tile([P, R], U32, name="wu_codes", align_bytes=64)
         wu_sc = keep.tile([P, R], U8, name="wu_sc", align_bytes=64)
         nc.vector.quantize_mx(wu_codes[:].bitcast(FP8X4), wu_sc[:], wu_bf[:])
-
-        v_codes = []
-        for g in range(J // PIECE):
-            codes = keep.tile([P, PIECE], U32, name="v_codes", tag=f"v_codes{g}", align_bytes=64)
-            nc.vector.tensor_copy(codes[:], tab_codes[:].bitcast(U32).indirect(offsets[:, g * PIECE // 16 : (g + 1) * PIECE // 16]))
-            v_codes.append(codes)
 
         gT_rows = gT.rearrange("(p t) c -> t p c", t=PACK)
         gates = [keep.tile([P, T], F32, name="gate", tag=f"gate{t}", align_bytes=64) for t in range(PACK)]
@@ -119,8 +118,9 @@ def tile_list_modp_ggelu_gateP_kernel(
 
         def product(n, bank, w_codes, w_dtype, width, w_sc):
             acc = psum.tile([P, PACK, CHUNK], F32, name="acc", tag=bank)
-            piece = v_codes[n * CHUNK // PIECE]
-            first = n * CHUNK % PIECE
+            g = max(i for i, lo in enumerate(WORD_EDGES[:-1]) if lo <= n * CHUNK)
+            piece = v_codes[g]
+            first = n * CHUNK - WORD_EDGES[g]
             for t in range(PACK):
                 nc.tensor.matmul_mx(
                     acc[:, t, :],
@@ -140,28 +140,29 @@ def tile_list_modp_ggelu_gateP_kernel(
             return act
 
         gws = {t: picked_gate(t) for t in range(STRAIGHT, PACK)}
-        h_codes = keep.tile([P, J], U32, name="h_codes", align_bytes=64)
         h_sc = keep.tile([P, J], U8, name="h_sc", align_bytes=64)
+        starts = ["tab_codes", "gate2", "gate3"]
         h_parts = []
         for lo, hi in zip(H_EDGES, H_EDGES[1:]):
-            h_bf = keep.tile([P, (hi - lo) * CHUNK, PACK], BF16, name="h_bf", tag=f"h_bf{lo}", align_bytes=64)
+            h_bf = keep.tile([P, (hi - lo) * CHUNK, PACK], BF16, name="h_bf", tag=starts[lo] if lo < GPSIMD_CHUNKS else f"h_bf{lo}", align_bytes=64)
             h_parts.append(h_bf)
             for n in range(lo, hi):
                 act = gelu_chunk(n)
                 ub = product(n, f"ub{n % STAGE_BANKS}", wu_codes, FP8X4, P, wu_sc)
                 h_chunk = h_bf[:, (n - lo) * CHUNK : (n - lo + 1) * CHUNK, :]
-                if lo == H_EDGES[-2]:
+                if n >= GPSIMD_CHUNKS:
                     nc.vector.tensor_tensor(h_chunk, ub[:].rearrange("p t j -> p j t"), act[:], MULT)
                 else:
                     ub_sb = keep.tile([P, CHUNK, PACK], F32, name="ub_sb", tag=f"ub_sb{n}", align_bytes=64)
                     nc.scalar.copy(ub_sb[:], ub[:].rearrange("p t j -> p j t"))
                     nc.gpsimd.tensor_tensor(h_chunk, ub_sb[:], act[:], MULT)
+        h_codes = keep.tile([P, J], U32, name="h_codes", tag="act6", align_bytes=64)
         for lo, hi, h_bf in zip(H_EDGES, H_EDGES[1:], h_parts):
             cols = slice(lo * CHUNK, hi * CHUNK)
             nc.vector.quantize_mx(h_codes[:, cols].bitcast(FP8X4), h_sc[:, cols], h_bf[:].rearrange("p j t -> p (j t)"))
 
         wd_codes = keep.tile([P, N], U32, name="wd_codes", align_bytes=64)
-        wd_bf = keep.tile([P, PACK * N], BF16, name="wd_bf", tag=f"v_codes{J // PIECE - 1}", align_bytes=64)
+        wd_bf = keep.tile([P, PACK * N], BF16, name="wd_bf", tag="v_codes1", align_bytes=64)
         nc.scalar.copy(
             wd_bf[:].rearrange("p (t m s) -> p m s t", t=PACK, s=PACK),
             wd_raw[:].rearrange("p s (m t) -> p m s t", t=PACK),
@@ -227,11 +228,11 @@ def tile_list_modp_ggelu_gateP_kernel(
         for t in range(PACK):
             if 0 < t < STRAIGHT:
                 gws[t] = picked_gate(t)
-            if t == PAGES:
-                third = keep.tile([P, T], F32, name="third", tag="gate0", align_bytes=64)
-                nc.gpsimd.memset(third[:], 0.0)
-                pages.append(third)
-            page = pages[t % (PAGES + 1)]
+            if 0 < t < PAGES:
+                fresh = keep.tile([P, T], F32, name="fresh", tag=f"gate{t - 1}", align_bytes=64)
+                nc.gpsimd.memset(fresh[:], 0.0)
+                pages.append(fresh)
+            page = pages[t % PAGES]
             nc.vector.tensor_tensor(page[:].indirect(offsets[:]), ys[t][:], gws[t][:], MULT)
             nc.sync.dma_start(out_rows[t], page[:])
             if t < PACK - 2:

@@ -15,19 +15,19 @@ U8 = mybir.dt.uint8
 FP8X4 = mybir.dt.float8_e4m3fn_x4
 FP4X4 = mybir.dt.float4_e2m1fn_x4
 MULT = mybir.AluOpType.mult
-COPY = mybir.ActivationFunctionType.Copy
 GELU = mybir.ActivationFunctionType.Gelu_apprx_tanh
 
 P = 128
 PACK = 4
+RUN = 8
+BLOCKS = P // RUN
 HALF = 512
 CHUNK = 128
 WORD_EDGES = [0, 256, 1024]
-PAGES = 3
 STAGE_BANKS = 4
-H_EDGES = [0, 1, 2, 3, 4, 8]
-GPSIMD_CHUNKS = 3
-STRAIGHT = 2
+H_EDGES = [0, 2, 4, 8]
+GPSIMD_CHUNKS = 2
+SLOT_ORDER = [0, 2, 1, 3]
 SPAN_EDGES = [0, 512, 1024, 1536, 1792, 2048]
 VECTOR_SPANS = 2
 
@@ -52,6 +52,8 @@ def tile_list_modp_ggelu_gateP_kernel(
         nc.vector.memset(first_page[:].bitcast(I32), 0)
         pages = [first_page]
 
+        wgo_rows = keep.tile([P, J // P], F32, name="wgo_rows", align_bytes=64)
+        nc.sync.dma_start(wgo_rows[:], wgo[0].rearrange("(n m) -> n m", n=P))
         wg_raw = keep.tile([P, R // 2], I32, name="wg_raw", align_bytes=64)
         nc.sync.dma_start(wg_raw[:], wg_words[0].bitcast(I32))
         for q in range(4):
@@ -61,59 +63,70 @@ def tile_list_modp_ggelu_gateP_kernel(
         for q in range(4):
             nc.sync.dma_start(wg_plane[32 * q : 32 * q + 4, :].bitcast(I32), wg_scales[0, 4 * q : 4 * q + 4, :].bitcast(I32))
         wu_rows = wu.rearrange("(p j) c -> p j c", j=PACK)
-        wu_lo = keep.tile([P, PACK, R // 2], F32, name="wu_lo", tag="act1", align_bytes=64)
-        nc.sync.dma_start(wu_lo[:], wu_rows[:, :, : R // 2])
-        wu_hi = keep.tile([P, PACK, R // 2], F32, name="wu_hi", align_bytes=64)
-        nc.sync.dma_start(wu_hi[:], wu_rows[:, :, R // 2 :])
-
-        v_sc = keep.tile([P, J], U8, name="v_sc", align_bytes=64)
-        nc.vector.tensor_copy(v_sc[:], tab_plane[:].indirect(offsets[:]))
-
-        wg_codes = keep.tile([P, 2 * R], U8, name="wg_codes", align_bytes=64)
-        wg_sc = keep.tile([P, R], U8, name="wg_sc", align_bytes=64)
-        nc.vector.tensor_copy(
-            wg_codes[:].bitcast(U16).rearrange("p (t m) -> p t m", t=PACK),
-            wg_raw[:].bitcast(U16).rearrange("p (m t) -> p t m", t=PACK),
-        )
-        nc.vector.tensor_copy(
-            wg_sc[:].rearrange("p (t m) -> p t m", t=PACK),
-            wg_plane[:].rearrange("p (m t) -> p t m", t=PACK),
-        )
-
-        v_codes = []
-        for g, (lo, hi) in enumerate(zip(WORD_EDGES, WORD_EDGES[1:])):
-            codes = keep.tile([P, hi - lo], U32, name="v_codes", tag=f"v_codes{g}", align_bytes=64)
-            nc.vector.tensor_copy(codes[:], tab_codes[:].bitcast(U32).indirect(offsets[:, lo // 16 : hi // 16]))
-            v_codes.append(codes)
-
-        wu_bf = keep.tile([P, PACK * R], BF16, name="wu_bf", align_bytes=64)
-        wu_dealt = wu_bf[:].rearrange("p (t m j) -> p m j t", t=PACK, j=PACK)
-        nc.scalar.copy(wu_dealt[:, : P // 2], wu_lo[:].rearrange("p j (m t) -> p m j t", t=PACK))
-        nc.vector.tensor_copy(wu_dealt[:, P // 2 :], wu_hi[:].rearrange("p j (m t) -> p m j t", t=PACK))
-        wu_codes = keep.tile([P, R], U32, name="wu_codes", align_bytes=64)
-        wu_sc = keep.tile([P, R], U8, name="wu_sc", align_bytes=64)
-        nc.vector.quantize_mx(wu_codes[:].bitcast(FP8X4), wu_sc[:], wu_bf[:])
+        wu_halves = []
+        for h, tag in enumerate(("wu_lo", "act1")):
+            wu_raw = keep.tile([P, PACK, R // 2], F32, name="wu_raw", tag=tag, align_bytes=64)
+            nc.sync.dma_start(wu_raw[:], wu_rows[:, :, h * (R // 2) : (h + 1) * (R // 2)])
+            wu_halves.append(wu_raw)
 
         gT_rows = gT.rearrange("(p t) c -> t p c", t=PACK)
         gates = [keep.tile([P, T], F32, name="gate", tag=f"gate{t}", align_bytes=64) for t in range(PACK)]
         wd_raw = keep.tile([P, PACK, N], F32, name="wd_raw", align_bytes=64)
         wgo_sb = keep.tile([P, J], F32, name="wgo_sb", tag="wgo", align_bytes=64)
-        for t in range(STRAIGHT, PACK):
+        wd_rows = wd.rearrange("(g t i) n -> t g i n", t=PACK, i=RUN)
+        nc.sync.dma_start(gates[SLOT_ORDER[0]][:], gT_rows[SLOT_ORDER[0]])
+        for t in range(PACK):
+            nc.sync.dma_start(wd_raw[:, t, :], wd_rows[t])
+        for t in SLOT_ORDER[1:]:
             nc.sync.dma_start(gates[t][:], gT_rows[t])
-        nc.sync.dma_start(wd_raw[:], wd.rearrange("(p s) n -> p s n", s=PACK))
-        nc.sync.dma_start(wgo_sb[:], wgo)
-        for t in range(STRAIGHT):
-            nc.sync.dma_start(gates[t][:], gT_rows[t])
-        wd_sc = keep.tile([P, N], U8, name="wd_sc", align_bytes=64)
+
         ident = keep.tile([P, P], F32, name="ident", align_bytes=64)
         make_identity(nc, ident[:])
+        wgo_runs = wgo_sb[:].rearrange("p (n m) -> p n m", n=P)
+        for h in range(J // HALF):
+            spread = psum.tile([P, PACK, P], F32, name="spread", tag=f"bank{6 + h}")
+            for i in range(PACK):
+                m = PACK * h + i
+                nc.tensor.transpose(spread[:, i, :], wgo_rows[:, m : m + 1].to_broadcast([P, P]), ident[:])
+            nc.scalar.copy(wgo_runs[:, :, PACK * h : PACK * (h + 1)], spread[:].rearrange("p m n -> p n m"))
 
-        def picked_gate(t):
-            gw = keep.tile([P, J], F32, name="gw", tag=f"gw{t}", align_bytes=64)
-            if t < STRAIGHT:
-                nc.vector.tensor_tensor(gw[:], gates[t][:].indirect(offsets[:]), wgo_sb[:], MULT)
-            else:
-                nc.vector.tensor_copy(gw[:], gates[t][:].indirect(offsets[:]))
+        v_sc = keep.tile([P, J], U8, name="v_sc", align_bytes=64)
+        nc.vector.tensor_copy(v_sc[:], tab_plane[:].indirect(offsets[:]))
+
+        def gather_words(g):
+            lo, hi = WORD_EDGES[g], WORD_EDGES[g + 1]
+            codes = keep.tile([P, hi - lo], U32, name="v_codes", tag=f"v_codes{g}", align_bytes=64)
+            nc.vector.tensor_copy(codes[:], tab_codes[:].bitcast(U32).indirect(offsets[:, lo // 16 : hi // 16]))
+            return codes
+
+        wg_codes = keep.tile([P, R // 2], I32, name="wg_codes", align_bytes=64)
+        wg_sc = keep.tile([P, R], U8, name="wg_sc", align_bytes=64)
+        nc.vector.tensor_copy(
+            wg_codes[:].rearrange("p (t g w) -> p t g w", t=PACK, g=BLOCKS),
+            wg_raw[:].rearrange("p (g t w) -> p t g w", t=PACK, g=BLOCKS),
+        )
+        v_codes = [gather_words(0)]
+        nc.vector.tensor_copy(
+            wg_sc[:].bitcast(I32).rearrange("p (t g w) -> p t g w", t=PACK, g=BLOCKS),
+            wg_plane[:].bitcast(I32).rearrange("p (g t w) -> p t g w", t=PACK, g=BLOCKS),
+        )
+        v_codes.append(gather_words(1))
+
+        wu_bf = keep.tile([P, PACK * R], BF16, name="wu_bf", align_bytes=64)
+        wu_dealt = wu_bf[:].rearrange("p (t g i j) -> p t g i j", t=PACK, g=BLOCKS, j=PACK)
+        for h, wu_raw in enumerate(wu_halves):
+            rounding = nc.vector.tensor_copy if h == 0 else nc.scalar.copy
+            rounding(
+                wu_dealt[:, :, h * (BLOCKS // 2) : (h + 1) * (BLOCKS // 2)],
+                wu_raw[:].rearrange("p j (g t i) -> p t g i j", t=PACK, i=RUN),
+            )
+        wu_codes = keep.tile([P, R], U32, name="wu_codes", align_bytes=64)
+        wu_sc = keep.tile([P, R], U8, name="wu_sc", align_bytes=64)
+        nc.vector.quantize_mx(wu_codes[:].bitcast(FP8X4), wu_sc[:], wu_bf[:])
+
+        def picked_gate(t, tag):
+            gw = keep.tile([P, J], F32, name="gw", tag=tag, align_bytes=64)
+            nc.vector.tensor_tensor(gw[:], gates[t][:].indirect(offsets[:]), wgo_sb[:], MULT)
             return gw
 
         def product(n, bank, w_codes, w_dtype, width, w_sc):
@@ -133,113 +146,92 @@ def tile_list_modp_ggelu_gateP_kernel(
                 )
             return acc
 
-        def gelu_chunk(n):
-            ga = product(n, f"ga{n % STAGE_BANKS}", wg_codes, FP4X4, 2 * P, wg_sc)
-            act = keep.tile([P, CHUNK, PACK], F32, name="act", tag=f"act{n}", align_bytes=64)
-            nc.scalar.activation(act[:], ga[:].rearrange("p t j -> p j t"), GELU)
-            return act
+        gws = {SLOT_ORDER[0]: picked_gate(SLOT_ORDER[0], "gw0")}
+        first_act = keep.tile([P, CHUNK, PACK], F32, name="first_act", align_bytes=64)
+        later_acts = keep.tile([P, J // CHUNK - 1, CHUNK, PACK], F32, name="later_acts", tag="act1", align_bytes=64)
+        acts = [first_act[:]] + [later_acts[:, n] for n in range(J // CHUNK - 1)]
 
-        gws = {t: picked_gate(t) for t in range(STRAIGHT, PACK)}
+        def gelu_chunk(n):
+            ga = product(n, f"bank{n}", wg_codes[:].bitcast(U8), FP4X4, 2 * P, wg_sc)
+            nc.scalar.activation(acts[n], ga[:].rearrange("p t j -> p j t"), GELU)
+
+        h_parts = [
+            keep.tile([P, (hi - lo) * CHUNK, PACK], BF16, name="h_bf", tag=f"gate{SLOT_ORDER[0]}" if lo == 0 else f"h_bf{lo}", align_bytes=64)
+            for lo, hi in zip(H_EDGES, H_EDGES[1:])
+        ]
+
+        def h_chunk(n, bank):
+            g = max(i for i, lo in enumerate(H_EDGES[:-1]) if lo <= n)
+            dst = h_parts[g][:, (n - H_EDGES[g]) * CHUNK : (n - H_EDGES[g] + 1) * CHUNK, :]
+            ub = product(n, f"bank{bank}", wu_codes, FP8X4, P, wu_sc)
+            if n >= GPSIMD_CHUNKS:
+                nc.vector.tensor_tensor(dst, ub[:].rearrange("p t j -> p j t"), acts[n], MULT)
+            else:
+                ub_sb = keep.tile([P, CHUNK, PACK], F32, name="ub_sb", tag=f"ub_sb{n}", align_bytes=64)
+                nc.scalar.copy(ub_sb[:], ub[:].rearrange("p t j -> p j t"))
+                nc.gpsimd.tensor_tensor(dst, ub_sb[:], acts[n], MULT)
+
+        for n in range(J // CHUNK):
+            gelu_chunk(n)
+            if n in (4, 5):
+                h_chunk(n - 4, n - 4)
+        for n in range(GPSIMD_CHUNKS, J // CHUNK):
+            h_chunk(n, n % (J // CHUNK - GPSIMD_CHUNKS))
+
         h_sc = keep.tile([P, J], U8, name="h_sc", align_bytes=64)
-        starts = ["tab_codes", "gate2", "gate3"]
-        h_parts = []
-        for lo, hi in zip(H_EDGES, H_EDGES[1:]):
-            h_bf = keep.tile([P, (hi - lo) * CHUNK, PACK], BF16, name="h_bf", tag=starts[lo] if lo < GPSIMD_CHUNKS else f"h_bf{lo}", align_bytes=64)
-            h_parts.append(h_bf)
-            for n in range(lo, hi):
-                act = gelu_chunk(n)
-                ub = product(n, f"ub{n % STAGE_BANKS}", wu_codes, FP8X4, P, wu_sc)
-                h_chunk = h_bf[:, (n - lo) * CHUNK : (n - lo + 1) * CHUNK, :]
-                if n >= GPSIMD_CHUNKS:
-                    nc.vector.tensor_tensor(h_chunk, ub[:].rearrange("p t j -> p j t"), act[:], MULT)
-                else:
-                    ub_sb = keep.tile([P, CHUNK, PACK], F32, name="ub_sb", tag=f"ub_sb{n}", align_bytes=64)
-                    nc.scalar.copy(ub_sb[:], ub[:].rearrange("p t j -> p j t"))
-                    nc.gpsimd.tensor_tensor(h_chunk, ub_sb[:], act[:], MULT)
-        h_codes = keep.tile([P, J], U32, name="h_codes", tag="act6", align_bytes=64)
+        h_codes = keep.tile([P, J], U32, name="h_codes", align_bytes=64)
+        wd_codes = keep.tile([P, N], U32, name="wd_codes", align_bytes=64)
+        wd_sc = keep.tile([P, N], U8, name="wd_sc", align_bytes=64)
+
+        def quantise_wd(u, tag):
+            wd_bf = keep.tile([P, PACK * N // 2], BF16, name="wd_bf", tag=tag, align_bytes=64)
+            nc.scalar.copy(
+                wd_bf[:].rearrange("p (t m s) -> p m s t", t=2, s=PACK),
+                wd_raw[:].rearrange("p s (m t u) -> p u m s t", t=2, u=2)[:, u],
+            )
+            cols = slice(u * N // 2, (u + 1) * N // 2)
+            nc.vector.quantize_mx(wd_codes[:, cols].bitcast(FP8X4), wd_sc[:, cols], wd_bf[:])
+
+        quantise_wd(0, "v_codes1")
         for lo, hi, h_bf in zip(H_EDGES, H_EDGES[1:], h_parts):
             cols = slice(lo * CHUNK, hi * CHUNK)
             nc.vector.quantize_mx(h_codes[:, cols].bitcast(FP8X4), h_sc[:, cols], h_bf[:].rearrange("p j t -> p (j t)"))
 
-        wd_codes = keep.tile([P, N], U32, name="wd_codes", align_bytes=64)
-        wd_bf = keep.tile([P, PACK * N], BF16, name="wd_bf", tag="v_codes1", align_bytes=64)
-        nc.scalar.copy(
-            wd_bf[:].rearrange("p (t m s) -> p m s t", t=PACK, s=PACK),
-            wd_raw[:].rearrange("p s (m t) -> p m s t", t=PACK),
-        )
-        nc.vector.quantize_mx(wd_codes[:].bitcast(FP8X4), wd_sc[:], wd_bf[:])
+        gws[SLOT_ORDER[1]] = picked_gate(SLOT_ORDER[1], "v_codes1")
+        gws[SLOT_ORDER[2]] = picked_gate(SLOT_ORDER[2], "gw2")
+        quantise_wd(1, "v_codes0")
+        second_page = keep.tile([P, T], F32, name="second_page", tag=f"gate{SLOT_ORDER[1]}", align_bytes=64)
+        nc.gpsimd.memset(second_page[:], 0.0)
+        pages.append(second_page)
 
-        gws[0] = picked_gate(0)
-
-        banks = [f"{kind}{b}" for kind in ("ga", "ub") for b in range(STAGE_BANKS)]
-        per_bank = HALF // P
-        wgo_col = keep.tile([P, J // P], F32, name="wgo_col", align_bytes=64)
-        for h in range(halves):
-            col_ps = psum.tile([P, per_bank, P], F32, name="col_ps", tag=banks[h])
-            for i in range(per_bank):
-                b = h * per_bank + i
-                nc.tensor.transpose(col_ps[:, i, :], wgo_sb[:, P * b : P * (b + 1)], ident[:])
-            nc.scalar.copy(wgo_col[:, h * per_bank : (h + 1) * per_bank], col_ps[:, :, 0])
-
-        ys = [keep.tile([P, J], F32, name=f"y{t}") for t in range(PACK)]
-        for t in range(STRAIGHT):
+        banks = [f"bank{b}" for b in range(8)]
+        ys = {}
+        for i, t in enumerate(SLOT_ORDER):
+            ys[t] = keep.tile([P, J], F32, name=f"y{t}")
             for h in range(halves):
-                y_ps = psum.tile([P, HALF], F32, name="y_ps", tag=banks[2 + halves * t + h])
+                y_ps = psum.tile([P, HALF], F32, name="y_ps", tag=banks[halves * i + h])
                 nc.tensor.matmul_mx(
                     y_ps[:],
-                    lhsT=wd_codes[:, P * t : P * (t + 1)].bitcast(FP8X4),
-                    lhsT_scale=wd_sc[:, P * t : P * (t + 1)],
+                    lhsT=wd_codes[:, P * i : P * (i + 1)].bitcast(FP8X4),
+                    lhsT_scale=wd_sc[:, P * i : P * (i + 1)],
                     rhs=h_codes[:, h * HALF : (h + 1) * HALF].bitcast(FP8X4),
                     rhs_scale=h_sc[:, h * HALF : (h + 1) * HALF],
                     start=True,
                     stop=True,
                 )
                 nc.scalar.copy(ys[t][:, h * HALF : (h + 1) * HALF], y_ps[:])
-        turned = PACK - STRAIGHT
-        y_tok = keep.tile([P, J // P, turned * P], F32, name="y_tok", tag="y_tok", align_bytes=64)
-        pair = HALF // (turned * P)
-        for g in range(J // P // pair):
-            tok_ps = psum.tile([P, pair, turned * P], F32, name="tok_ps", tag=banks[(6 + g) % len(banks)])
-            for i in range(pair):
-                b = g * pair + i
-                nc.tensor.matmul_mx(
-                    tok_ps[:, i, :],
-                    lhsT=h_codes[:, P * b : P * (b + 1)].bitcast(FP8X4),
-                    lhsT_scale=h_sc[:, P * b : P * (b + 1)],
-                    rhs=wd_codes[:, P * STRAIGHT :].bitcast(FP8X4),
-                    rhs_scale=wd_sc[:, P * STRAIGHT :],
-                    start=True,
-                    stop=True,
-                )
-            for i in range(pair):
-                b = g * pair + i
-                nc.scalar.activation(y_tok[:, b, :], tok_ps[:, i, :], COPY, scale=wgo_col[:, b : b + 1])
-        for t in range(STRAIGHT, PACK):
-            for h in range(halves):
-                back_ps = psum.tile([P, per_bank, P], F32, name="back_ps", tag=banks[2 + halves * (t - STRAIGHT) + h])
-                for i in range(per_bank):
-                    nc.tensor.transpose(back_ps[:, i, :], y_tok[:, h * per_bank + i, P * (t - STRAIGHT) : P * (t - STRAIGHT + 1)], ident[:])
-                nc.scalar.copy(ys[t][:, h * HALF : (h + 1) * HALF], back_ps[:].rearrange("p i j -> p (i j)"))
 
-        out_bf = keep.tile([P, T, PACK], BF16, name="out_bf", tag="y_tok", align_bytes=64)
+        out_bf = keep.tile([P, T, PACK], BF16, name="out_bf", align_bytes=64)
         out_rows = out_0.rearrange("(p t) c -> t p c", t=PACK)
         spans = [slice(lo, hi) for lo, hi in zip(SPAN_EDGES, SPAN_EDGES[1:])]
-        shared = SPAN_EDGES[VECTOR_SPANS]
-        for t in range(PACK):
-            if 0 < t < STRAIGHT:
-                gws[t] = picked_gate(t)
-            if 0 < t < PAGES:
-                fresh = keep.tile([P, T], F32, name="fresh", tag=f"gate{t - 1}", align_bytes=64)
-                nc.gpsimd.memset(fresh[:], 0.0)
-                pages.append(fresh)
-            page = pages[t % PAGES]
+        for i, t in enumerate(SLOT_ORDER):
+            if i == PACK - 2:
+                gws[SLOT_ORDER[-1]] = picked_gate(SLOT_ORDER[-1], "gw0")
+            page = pages[i % 2]
             nc.vector.tensor_tensor(page[:].indirect(offsets[:]), ys[t][:], gws[t][:], MULT)
             nc.sync.dma_start(out_rows[t], page[:])
-            if t < PACK - 2:
+            if i < PACK - 1:
                 nc.scalar.copy(out_bf[:, :, t], page[:])
-            elif t == PACK - 2:
-                nc.scalar.copy(out_bf[:, :shared, t : t + 2], page[:, :shared].unsqueeze(2).to_broadcast([P, shared, 2]))
-                nc.scalar.copy(out_bf[:, shared:, t], page[:, shared:])
             else:
                 for a, s in enumerate(spans):
                     if a < VECTOR_SPANS:

@@ -25,6 +25,7 @@ HALF = 512
 CHUNK = 128
 WORD_EDGES = [0, 256, 1024]
 STAGE_BANKS = 4
+WU_EDGES = [0, 8, 16]
 H_EDGES = [0, 2, 4, 8]
 GPSIMD_CHUNKS = 2
 SLOT_ORDER = [0, 2, 1, 3]
@@ -62,22 +63,23 @@ def tile_list_modp_ggelu_gateP_kernel(
         nc.sync.dma_start(tab_codes[:], tab_words[0].rearrange("p t i -> p (t i)").bitcast(I32))
         for q in range(4):
             nc.sync.dma_start(wg_plane[32 * q : 32 * q + 4, :].bitcast(I32), wg_scales[0, 4 * q : 4 * q + 4, :].bitcast(I32))
-        wu_rows = wu.rearrange("(p j) c -> p j c", j=PACK)
-        wu_halves = []
-        for h, tag in enumerate(("wu_lo", "act1")):
-            wu_raw = keep.tile([P, PACK, R // 2], F32, name="wu_raw", tag=tag, align_bytes=64)
-            nc.sync.dma_start(wu_raw[:], wu_rows[:, :, h * (R // 2) : (h + 1) * (R // 2)])
-            wu_halves.append(wu_raw)
-
         gT_rows = gT.rearrange("(p t) c -> t p c", t=PACK)
         gates = [keep.tile([P, T], F32, name="gate", tag=f"gate{t}", align_bytes=64) for t in range(PACK)]
         wd_raw = keep.tile([P, PACK, N], F32, name="wd_raw", align_bytes=64)
         wgo_sb = keep.tile([P, J], F32, name="wgo_sb", tag="wgo", align_bytes=64)
         wd_rows = wd.rearrange("(g t i) n -> t g i n", t=PACK, i=RUN)
         nc.sync.dma_start(gates[SLOT_ORDER[0]][:], gT_rows[SLOT_ORDER[0]])
+        wu_rows = wu.rearrange("(p j) c -> p j c", j=PACK)
+        wu_halves = []
+        for lo, hi, tag in zip(WU_EDGES, WU_EDGES[1:], ("wu_lo", "wu_hi")):
+            wu_raw = keep.tile([P, PACK, 32 * (hi - lo)], F32, name="wu_raw", tag=tag, align_bytes=64)
+            nc.sync.dma_start(wu_raw[:], wu_rows[:, :, 32 * lo : 32 * hi])
+            wu_halves.append(wu_raw)
+
+        nc.sync.dma_start(gates[SLOT_ORDER[1]][:], gT_rows[SLOT_ORDER[1]])
         for t in range(PACK):
             nc.sync.dma_start(wd_raw[:, t, :], wd_rows[t])
-        for t in SLOT_ORDER[1:]:
+        for t in SLOT_ORDER[2:]:
             nc.sync.dma_start(gates[t][:], gT_rows[t])
 
         ident = keep.tile([P, P], F32, name="ident", align_bytes=64)
@@ -112,22 +114,24 @@ def tile_list_modp_ggelu_gateP_kernel(
         )
         v_codes.append(gather_words(1))
 
+        def picked_gate(t, tag):
+            gw = keep.tile([P, J], F32, name="gw", tag=tag, align_bytes=64)
+            nc.vector.tensor_tensor(gw[:], gates[t][:].indirect(offsets[:]), wgo_sb[:], MULT)
+            return gw
+
+        gws = {SLOT_ORDER[0]: picked_gate(SLOT_ORDER[0], "gw0")}
+
         wu_bf = keep.tile([P, PACK * R], BF16, name="wu_bf", align_bytes=64)
         wu_dealt = wu_bf[:].rearrange("p (t g i j) -> p t g i j", t=PACK, g=BLOCKS, j=PACK)
         for h, wu_raw in enumerate(wu_halves):
-            rounding = nc.vector.tensor_copy if h == 0 else nc.scalar.copy
+            rounding = nc.scalar.copy if h == 0 else nc.vector.tensor_copy
             rounding(
-                wu_dealt[:, :, h * (BLOCKS // 2) : (h + 1) * (BLOCKS // 2)],
+                wu_dealt[:, :, WU_EDGES[h] : WU_EDGES[h + 1]],
                 wu_raw[:].rearrange("p j (g t i) -> p t g i j", t=PACK, i=RUN),
             )
         wu_codes = keep.tile([P, R], U32, name="wu_codes", align_bytes=64)
         wu_sc = keep.tile([P, R], U8, name="wu_sc", align_bytes=64)
         nc.vector.quantize_mx(wu_codes[:].bitcast(FP8X4), wu_sc[:], wu_bf[:])
-
-        def picked_gate(t, tag):
-            gw = keep.tile([P, J], F32, name="gw", tag=tag, align_bytes=64)
-            nc.vector.tensor_tensor(gw[:], gates[t][:].indirect(offsets[:]), wgo_sb[:], MULT)
-            return gw
 
         def product(n, bank, w_codes, w_dtype, width, w_sc):
             acc = psum.tile([P, PACK, CHUNK], F32, name="acc", tag=bank)
@@ -146,17 +150,21 @@ def tile_list_modp_ggelu_gateP_kernel(
                 )
             return acc
 
-        gws = {SLOT_ORDER[0]: picked_gate(SLOT_ORDER[0], "gw0")}
-        first_act = keep.tile([P, CHUNK, PACK], F32, name="first_act", align_bytes=64)
-        later_acts = keep.tile([P, J // CHUNK - 1, CHUNK, PACK], F32, name="later_acts", tag="act1", align_bytes=64)
-        acts = [first_act[:]] + [later_acts[:, n] for n in range(J // CHUNK - 1)]
+        gws[SLOT_ORDER[1]] = picked_gate(SLOT_ORDER[1], "gw1")
+        second_page = keep.tile([P, T], F32, name="second_page", tag="wu_bf", align_bytes=64)
+        nc.gpsimd.memset(second_page[:], 0.0)
+        pages.append(second_page)
+        early = WORD_EDGES[1] // CHUNK
+        first_acts = keep.tile([P, early, CHUNK, PACK], F32, name="first_acts", align_bytes=64)
+        later_acts = keep.tile([P, J // CHUNK - early, CHUNK, PACK], F32, name="later_acts", tag="wu_lo", align_bytes=64)
+        acts = [first_acts[:, n] for n in range(early)] + [later_acts[:, n] for n in range(J // CHUNK - early)]
 
         def gelu_chunk(n):
             ga = product(n, f"bank{n}", wg_codes[:].bitcast(U8), FP4X4, 2 * P, wg_sc)
             nc.scalar.activation(acts[n], ga[:].rearrange("p t j -> p j t"), GELU)
 
         h_parts = [
-            keep.tile([P, (hi - lo) * CHUNK, PACK], BF16, name="h_bf", tag=f"gate{SLOT_ORDER[0]}" if lo == 0 else f"h_bf{lo}", align_bytes=64)
+            keep.tile([P, (hi - lo) * CHUNK, PACK], BF16, name="h_bf", tag=f"gate{SLOT_ORDER[1]}" if lo == 0 else f"h_bf{lo}", align_bytes=64)
             for lo, hi in zip(H_EDGES, H_EDGES[1:])
         ]
 
@@ -173,36 +181,27 @@ def tile_list_modp_ggelu_gateP_kernel(
 
         for n in range(J // CHUNK):
             gelu_chunk(n)
-            if n in (4, 5):
-                h_chunk(n - 4, n - 4)
+            if n >= J // CHUNK - 1 - GPSIMD_CHUNKS and n < J // CHUNK - 1:
+                h_chunk(n - 5, n - 5)
         for n in range(GPSIMD_CHUNKS, J // CHUNK):
-            h_chunk(n, n % (J // CHUNK - GPSIMD_CHUNKS))
+            h_chunk(n, n)
 
         h_sc = keep.tile([P, J], U8, name="h_sc", align_bytes=64)
         h_codes = keep.tile([P, J], U32, name="h_codes", align_bytes=64)
         wd_codes = keep.tile([P, N], U32, name="wd_codes", align_bytes=64)
         wd_sc = keep.tile([P, N], U8, name="wd_sc", align_bytes=64)
 
-        def quantise_wd(u, tag):
-            wd_bf = keep.tile([P, PACK * N // 2], BF16, name="wd_bf", tag=tag, align_bytes=64)
-            nc.scalar.copy(
-                wd_bf[:].rearrange("p (t m s) -> p m s t", t=2, s=PACK),
-                wd_raw[:].rearrange("p s (m t u) -> p u m s t", t=2, u=2)[:, u],
-            )
-            cols = slice(u * N // 2, (u + 1) * N // 2)
-            nc.vector.quantize_mx(wd_codes[:, cols].bitcast(FP8X4), wd_sc[:, cols], wd_bf[:])
-
-        quantise_wd(0, "v_codes1")
+        wd_bf = keep.tile([P, PACK * N], BF16, name="wd_bf", align_bytes=64)
+        nc.scalar.copy(
+            wd_bf[:].rearrange("p (t m s) -> p m s t", t=PACK, s=PACK),
+            wd_raw[:].rearrange("p s (m t) -> p m s t", t=PACK),
+        )
+        nc.vector.quantize_mx(wd_codes[:].bitcast(FP8X4), wd_sc[:], wd_bf[:])
         for lo, hi, h_bf in zip(H_EDGES, H_EDGES[1:], h_parts):
             cols = slice(lo * CHUNK, hi * CHUNK)
             nc.vector.quantize_mx(h_codes[:, cols].bitcast(FP8X4), h_sc[:, cols], h_bf[:].rearrange("p j t -> p (j t)"))
 
-        gws[SLOT_ORDER[1]] = picked_gate(SLOT_ORDER[1], "v_codes1")
-        gws[SLOT_ORDER[2]] = picked_gate(SLOT_ORDER[2], "gw2")
-        quantise_wd(1, "v_codes0")
-        second_page = keep.tile([P, T], F32, name="second_page", tag=f"gate{SLOT_ORDER[1]}", align_bytes=64)
-        nc.gpsimd.memset(second_page[:], 0.0)
-        pages.append(second_page)
+        gws[SLOT_ORDER[2]] = picked_gate(SLOT_ORDER[2], "h_bf2")
 
         banks = [f"bank{b}" for b in range(8)]
         ys = {}
@@ -212,8 +211,8 @@ def tile_list_modp_ggelu_gateP_kernel(
                 y_ps = psum.tile([P, HALF], F32, name="y_ps", tag=banks[halves * i + h])
                 nc.tensor.matmul_mx(
                     y_ps[:],
-                    lhsT=wd_codes[:, P * i : P * (i + 1)].bitcast(FP8X4),
-                    lhsT_scale=wd_sc[:, P * i : P * (i + 1)],
+                    lhsT=wd_codes[:, P * t : P * (t + 1)].bitcast(FP8X4),
+                    lhsT_scale=wd_sc[:, P * t : P * (t + 1)],
                     rhs=h_codes[:, h * HALF : (h + 1) * HALF].bitcast(FP8X4),
                     rhs_scale=h_sc[:, h * HALF : (h + 1) * HALF],
                     start=True,

@@ -23,7 +23,7 @@ RUN = 8
 BLOCKS = P // RUN
 HALF = 512
 CHUNK = 128
-WORD_EDGES = [0, 256, 1024]
+WORD_EDGES = [0, 384, 1024]
 STAGE_BANKS = 4
 WU_EDGES = [0, 8, 16]
 H_EDGES = [0, 2, 4, 8]
@@ -31,6 +31,8 @@ GPSIMD_CHUNKS = 2
 SLOT_ORDER = [0, 2, 1, 3]
 SPAN_EDGES = [0, 512, 1024, 1536, 1792, 2048]
 VECTOR_SPANS = 2
+QUARTER = T // 4
+PIECE = 256
 
 
 def tile_list_modp_ggelu_gateP_kernel(
@@ -46,7 +48,7 @@ def tile_list_modp_ggelu_gateP_kernel(
         nc.sync.dma_start(offsets[:], offs)
 
         tab_plane = keep.tile([P, T], U8, name="tab_plane", align_bytes=64)
-        wg_plane = keep.tile([P, R], U8, name="wg_plane", tag="v_codes1", align_bytes=64)
+        wg_plane = keep.tile([P, R], U8, name="wg_plane", align_bytes=64)
         nc.vector.memset(tab_plane[:].bitcast(I32), 0)
         nc.vector.memset(wg_plane[:].bitcast(I32), 0)
         first_page = keep.tile([P, T], F32, name="first_page")
@@ -55,12 +57,18 @@ def tile_list_modp_ggelu_gateP_kernel(
 
         wgo_rows = keep.tile([P, J // P], F32, name="wgo_rows", align_bytes=64)
         nc.sync.dma_start(wgo_rows[:], wgo[0].rearrange("(n m) -> n m", n=P))
-        wg_raw = keep.tile([P, R // 2], I32, name="wg_raw", align_bytes=64)
-        nc.sync.dma_start(wg_raw[:], wg_words[0].bitcast(I32))
+        wu_rows = wu.rearrange("(p j) c -> p j c", j=PACK)
+        wu_halves = [
+            keep.tile([P, PACK, 32 * (hi - lo)], F32, name="wu_raw", tag=tag, align_bytes=64)
+            for lo, hi, tag in zip(WU_EDGES, WU_EDGES[1:], ("wu_lo", "wu_hi"))
+        ]
+        nc.sync.dma_start(wu_halves[0][:], wu_rows[:, :, : 32 * WU_EDGES[1]])
         for q in range(4):
             nc.sync.dma_start(tab_plane[32 * q : 32 * q + 4, :].bitcast(I32), tab_scales[0, 4 * q : 4 * q + 4, :].bitcast(I32))
         tab_codes = keep.tile([P, T], I32, name="tab_codes", align_bytes=64)
         nc.sync.dma_start(tab_codes[:], tab_words[0].rearrange("p t i -> p (t i)").bitcast(I32))
+        wg_raw = keep.tile([P, R // 2], I32, name="wg_raw", align_bytes=64)
+        nc.sync.dma_start(wg_raw[:], wg_words[0].bitcast(I32))
         for q in range(4):
             nc.sync.dma_start(wg_plane[32 * q : 32 * q + 4, :].bitcast(I32), wg_scales[0, 4 * q : 4 * q + 4, :].bitcast(I32))
         gT_rows = gT.rearrange("(p t) c -> t p c", t=PACK)
@@ -69,13 +77,7 @@ def tile_list_modp_ggelu_gateP_kernel(
         wgo_sb = keep.tile([P, J], F32, name="wgo_sb", tag="wgo", align_bytes=64)
         wd_rows = wd.rearrange("(g t i) n -> t g i n", t=PACK, i=RUN)
         nc.sync.dma_start(gates[SLOT_ORDER[0]][:], gT_rows[SLOT_ORDER[0]])
-        wu_rows = wu.rearrange("(p j) c -> p j c", j=PACK)
-        wu_halves = []
-        for lo, hi, tag in zip(WU_EDGES, WU_EDGES[1:], ("wu_lo", "wu_hi")):
-            wu_raw = keep.tile([P, PACK, 32 * (hi - lo)], F32, name="wu_raw", tag=tag, align_bytes=64)
-            nc.sync.dma_start(wu_raw[:], wu_rows[:, :, 32 * lo : 32 * hi])
-            wu_halves.append(wu_raw)
-
+        nc.sync.dma_start(wu_halves[1][:], wu_rows[:, :, 32 * WU_EDGES[1] :])
         nc.sync.dma_start(gates[SLOT_ORDER[1]][:], gT_rows[SLOT_ORDER[1]])
         for t in range(PACK):
             nc.sync.dma_start(wd_raw[:, t, :], wd_rows[t])
@@ -103,12 +105,12 @@ def tile_list_modp_ggelu_gateP_kernel(
 
         wg_codes = keep.tile([P, R // 2], I32, name="wg_codes", align_bytes=64)
         wg_sc = keep.tile([P, R], U8, name="wg_sc", align_bytes=64)
-        nc.vector.tensor_copy(
+        nc.gpsimd.tensor_copy(
             wg_codes[:].rearrange("p (t g w) -> p t g w", t=PACK, g=BLOCKS),
             wg_raw[:].rearrange("p (g t w) -> p t g w", t=PACK, g=BLOCKS),
         )
         v_codes = [gather_words(0)]
-        nc.vector.tensor_copy(
+        nc.gpsimd.tensor_copy(
             wg_sc[:].bitcast(I32).rearrange("p (t g w) -> p t g w", t=PACK, g=BLOCKS),
             wg_plane[:].bitcast(I32).rearrange("p (g t w) -> p t g w", t=PACK, g=BLOCKS),
         )
@@ -124,8 +126,7 @@ def tile_list_modp_ggelu_gateP_kernel(
         wu_bf = keep.tile([P, PACK * R], BF16, name="wu_bf", align_bytes=64)
         wu_dealt = wu_bf[:].rearrange("p (t g i j) -> p t g i j", t=PACK, g=BLOCKS, j=PACK)
         for h, wu_raw in enumerate(wu_halves):
-            rounding = nc.scalar.copy if h == 0 else nc.vector.tensor_copy
-            rounding(
+            nc.scalar.copy(
                 wu_dealt[:, :, WU_EDGES[h] : WU_EDGES[h + 1]],
                 wu_raw[:].rearrange("p j (g t i) -> p t g i j", t=PACK, i=RUN),
             )
@@ -156,7 +157,7 @@ def tile_list_modp_ggelu_gateP_kernel(
         pages.append(second_page)
         early = WORD_EDGES[1] // CHUNK
         first_acts = keep.tile([P, early, CHUNK, PACK], F32, name="first_acts", align_bytes=64)
-        later_acts = keep.tile([P, J // CHUNK - early, CHUNK, PACK], F32, name="later_acts", tag="wu_lo", align_bytes=64)
+        later_acts = keep.tile([P, J // CHUNK - early, CHUNK, PACK], F32, name="later_acts", tag="wu_hi", align_bytes=64)
         acts = [first_acts[:, n] for n in range(early)] + [later_acts[:, n] for n in range(J // CHUNK - early)]
 
         def gelu_chunk(n):
@@ -238,12 +239,18 @@ def tile_list_modp_ggelu_gateP_kernel(
                     else:
                         nc.scalar.copy(out_bf[:, s, t], page[:, s])
 
-        out_sc = keep.tile([P, T], U8, name="out_sc", align_bytes=64)
+        out_sc = keep.tile([P, QUARTER], U8, name="out_sc", align_bytes=64)
         out_codes = keep.tile([P, T], I32, name="out_codes", align_bytes=64)
         out_words = out_1[0].rearrange("p t i -> p (t i)").bitcast(I32)
         for s in spans:
-            nc.vector.quantize_mx(out_codes[:, s].bitcast(FP8X4), out_sc[:, s], out_bf[:, s, :].rearrange("p c t -> p (c t)"))
+            for lo in range(s.start, s.stop, PIECE):
+                cols = slice(lo, lo + PIECE)
+                plane = out_sc[4 * (lo // QUARTER) :, lo % QUARTER : lo % QUARTER + PIECE]
+                nc.vector.quantize_mx(out_codes[:, cols].bitcast(FP8X4), plane, out_bf[:, cols, :].rearrange("p c t -> p (c t)"))
             nc.sync.dma_start(out_words[:, s], out_codes[:, s])
         for q in range(4):
             queue = nc.scalar if q % 2 == 0 else nc.sync
-            queue.dma_start(out_2[0, 4 * q : 4 * q + 4, :].bitcast(I32), out_sc[32 * q : 32 * q + 4, :].bitcast(I32))
+            queue.dma_start(
+                out_2[0, 4 * q : 4 * q + 4, :].bitcast(I32).rearrange("r (k c) -> k r c", k=4),
+                out_sc[32 * q : 32 * q + 16, :].bitcast(I32),
+            )

@@ -23,7 +23,7 @@ RUN = 8
 BLOCKS = P // RUN
 HALF = 512
 CHUNK = 128
-WORD_EDGES = [0, 384, 1024]
+WORD_EDGES = [0, 256, 1024]
 STAGE_BANKS = 4
 WU_EDGES = [0, 8, 16]
 H_EDGES = [0, 2, 4, 8]

@@ -25,7 +25,7 @@ HALF = 512
 CHUNK = 128
 WORD_EDGES = [0, 256, 1024]
 STAGE_BANKS = 4
-WU_EDGES = [0, 8, 16]
+WU_EDGES = [0, 10, 16]
 H_EDGES = [0, 2, 4, 8]
 GPSIMD_CHUNKS = 2
 SLOT_ORDER = [0, 2, 1, 3]
@@ -44,6 +44,12 @@ def tile_list_modp_ggelu_gateP_kernel(
         keep = ctx.enter_context(tc.tile_pool(name="keep", bufs=1))
         psum = ctx.enter_context(tc.psum_pool(name="psum", bufs=1))
 
+        wu_rows = wu.rearrange("(p j) c -> p j c", j=PACK)
+        wu_halves = [
+            keep.tile([P, PACK, 32 * (hi - lo)], F32, name="wu_raw", tag=tag, align_bytes=64)
+            for lo, hi, tag in zip(WU_EDGES, WU_EDGES[1:], ("wu_lo", "wu_hi"))
+        ]
+        nc.sync.dma_start(wu_halves[0][:], wu_rows[:, :, : 32 * WU_EDGES[1]])
         offsets = keep.tile([P, J // 16], U16, name="offsets")
         nc.sync.dma_start(offsets[:], offs)
 
@@ -57,12 +63,6 @@ def tile_list_modp_ggelu_gateP_kernel(
 
         wgo_rows = keep.tile([P, J // P], F32, name="wgo_rows", align_bytes=64)
         nc.sync.dma_start(wgo_rows[:], wgo[0].rearrange("(n m) -> n m", n=P))
-        wu_rows = wu.rearrange("(p j) c -> p j c", j=PACK)
-        wu_halves = [
-            keep.tile([P, PACK, 32 * (hi - lo)], F32, name="wu_raw", tag=tag, align_bytes=64)
-            for lo, hi, tag in zip(WU_EDGES, WU_EDGES[1:], ("wu_lo", "wu_hi"))
-        ]
-        nc.sync.dma_start(wu_halves[0][:], wu_rows[:, :, : 32 * WU_EDGES[1]])
         for q in range(4):
             nc.sync.dma_start(tab_plane[32 * q : 32 * q + 4, :].bitcast(I32), tab_scales[0, 4 * q : 4 * q + 4, :].bitcast(I32))
         tab_codes = keep.tile([P, T], I32, name="tab_codes", align_bytes=64)

@@ -105,14 +105,14 @@ def tile_list_modp_ggelu_gateP_kernel(
 
         wg_codes = keep.tile([P, R // 2], I32, name="wg_codes", align_bytes=64)
         wg_sc = keep.tile([P, R], U8, name="wg_sc", align_bytes=64)
-        nc.gpsimd.tensor_copy(
-            wg_codes[:].rearrange("p (t g w) -> p t g w", t=PACK, g=BLOCKS),
-            wg_raw[:].rearrange("p (g t w) -> p t g w", t=PACK, g=BLOCKS),
+        nc.scalar.copy(
+            wg_codes[:].bitcast(U32).rearrange("p (t g w) -> p t g w", t=PACK, g=BLOCKS),
+            wg_raw[:].bitcast(U32).rearrange("p (g t w) -> p t g w", t=PACK, g=BLOCKS),
         )
         v_codes = [gather_words(0)]
-        nc.gpsimd.tensor_copy(
-            wg_sc[:].bitcast(I32).rearrange("p (t g w) -> p t g w", t=PACK, g=BLOCKS),
-            wg_plane[:].bitcast(I32).rearrange("p (g t w) -> p t g w", t=PACK, g=BLOCKS),
+        nc.scalar.copy(
+            wg_sc[:].bitcast(U32).rearrange("p (t g w) -> p t g w", t=PACK, g=BLOCKS),
+            wg_plane[:].bitcast(U32).rearrange("p (g t w) -> p t g w", t=PACK, g=BLOCKS),
         )
         v_codes.append(gather_words(1))
 

from contextlib import ExitStack

import concourse.mybir as mybir
from concourse.masks import make_identity

K, R, N, T, J = 512, 512, 512, 2048, 1024
FLOPS = 2 * J * (2 * K * R + R * N)

F32 = mybir.dt.float32
BF16 = mybir.dt.bfloat16
I32 = mybir.dt.int32
U32 = mybir.dt.uint32
U16 = mybir.dt.uint16
U8 = mybir.dt.uint8
FP8X4 = mybir.dt.float8_e4m3fn_x4
FP4X4 = mybir.dt.float4_e2m1fn_x4
MULT = mybir.AluOpType.mult
GELU = mybir.ActivationFunctionType.Gelu_apprx_tanh

P = 128
PACK = 4
RUN = 8
BLOCKS = P // RUN
HALF = 512
CHUNK = 128
WORD_EDGES = [0, 256, 1024]
STAGE_BANKS = 4
WU_EDGES = [0, 10, 16]
H_EDGES = [0, 2, 4, 8]
GPSIMD_CHUNKS = 2
SLOT_ORDER = [0, 2, 1, 3]
SPAN_EDGES = [0, 512, 1024, 1536, 1792, 2048]
VECTOR_SPANS = 2
QUARTER = T // 4
PIECE = 256


def tile_list_modp_ggelu_gateP_kernel(
    tc, tab_words, tab_scales, wg_words, wg_scales, wu, wd, gT, wgo, offs, out_0, out_1, out_2
):
    nc = tc.nc
    halves = J // HALF
    with ExitStack() as ctx:
        keep = ctx.enter_context(tc.tile_pool(name="keep", bufs=1))
        psum = ctx.enter_context(tc.psum_pool(name="psum", bufs=1))

        wu_rows = wu.rearrange("(p j) c -> p j c", j=PACK)
        wu_halves = [
            keep.tile([P, PACK, 32 * (hi - lo)], F32, name="wu_raw", tag=tag, align_bytes=64)
            for lo, hi, tag in zip(WU_EDGES, WU_EDGES[1:], ("wu_lo", "wu_hi"))
        ]
        nc.sync.dma_start(wu_halves[0][:], wu_rows[:, :, : 32 * WU_EDGES[1]])
        offsets = keep.tile([P, J // 16], U16, name="offsets")
        nc.sync.dma_start(offsets[:], offs)

        tab_plane = keep.tile([P, T], U8, name="tab_plane", align_bytes=64)
        wg_plane = keep.tile([P, R], U8, name="wg_plane", align_bytes=64)
        nc.vector.memset(tab_plane[:].bitcast(I32), 0)
        nc.vector.memset(wg_plane[:].bitcast(I32), 0)
        first_page = keep.tile([P, T], F32, name="first_page")
        nc.vector.memset(first_page[:].bitcast(I32), 0)
        pages = [first_page]

        wgo_rows = keep.tile([P, J // P], F32, name="wgo_rows", align_bytes=64)
        nc.sync.dma_start(wgo_rows[:], wgo[0].rearrange("(n m) -> n m", n=P))
        for q in range(4):
            nc.sync.dma_start(tab_plane[32 * q : 32 * q + 4, :].bitcast(I32), tab_scales[0, 4 * q : 4 * q + 4, :].bitcast(I32))
        tab_codes = keep.tile([P, T], I32, name="tab_codes", align_bytes=64)
        nc.sync.dma_start(tab_codes[:], tab_words[0].rearrange("p t i -> p (t i)").bitcast(I32))
        wg_raw = keep.tile([P, R // 2], I32, name="wg_raw", align_bytes=64)
        nc.sync.dma_start(wg_raw[:], wg_words[0].bitcast(I32))
        for q in range(4):
            nc.sync.dma_start(wg_plane[32 * q : 32 * q + 4, :].bitcast(I32), wg_scales[0, 4 * q : 4 * q + 4, :].bitcast(I32))
        gT_rows = gT.rearrange("(p t) c -> t p c", t=PACK)
        gates = [keep.tile([P, T], F32, name="gate", tag=f"gate{t}", align_bytes=64) for t in range(PACK)]
        wd_raw = keep.tile([P, PACK, N], F32, name="wd_raw", align_bytes=64)
        wgo_sb = keep.tile([P, J], F32, name="wgo_sb", tag="wgo", align_bytes=64)
        wd_rows = wd.rearrange("(g t i) n -> t g i n", t=PACK, i=RUN)
        nc.sync.dma_start(gates[SLOT_ORDER[0]][:], gT_rows[SLOT_ORDER[0]])
        nc.sync.dma_start(wu_halves[1][:], wu_rows[:, :, 32 * WU_EDGES[1] :])
        nc.sync.dma_start(gates[SLOT_ORDER[1]][:], gT_rows[SLOT_ORDER[1]])
        for t in range(PACK):
            nc.sync.dma_start(wd_raw[:, t, :], wd_rows[t])
        for t in SLOT_ORDER[2:]:
            nc.sync.dma_start(gates[t][:], gT_rows[t])

        ident = keep.tile([P, P], F32, name="ident", align_bytes=64)
        make_identity(nc, ident[:])
        wgo_runs = wgo_sb[:].rearrange("p (n m) -> p n m", n=P)
        for h in range(J // HALF):
            spread = psum.tile([P, PACK, P], F32, name="spread", tag=f"bank{6 + h}")
            for i in range(PACK):
                m = PACK * h + i
                nc.tensor.transpose(spread[:, i, :], wgo_rows[:, m : m + 1].to_broadcast([P, P]), ident[:])
            nc.scalar.copy(wgo_runs[:, :, PACK * h : PACK * (h + 1)], spread[:].rearrange("p m n -> p n m"))

        v_sc = keep.tile([P, J], U8, name="v_sc", align_bytes=64)
        nc.vector.tensor_copy(v_sc[:], tab_plane[:].indirect(offsets[:]))

        def gather_words(g):
            lo, hi = WORD_EDGES[g], WORD_EDGES[g + 1]
            codes = keep.tile([P, hi - lo], U32, name="v_codes", tag=f"v_codes{g}", align_bytes=64)
            nc.vector.tensor_copy(codes[:], tab_codes[:].bitcast(U32).indirect(offsets[:, lo // 16 : hi // 16]))
            return codes

        wg_codes = keep.tile([P, R // 2], I32, name="wg_codes", align_bytes=64)
        wg_sc = keep.tile([P, R], U8, name="wg_sc", align_bytes=64)
        nc.scalar.copy(
            wg_codes[:].bitcast(U32).rearrange("p (t g w) -> p t g w", t=PACK, g=BLOCKS),
            wg_raw[:].bitcast(U32).rearrange("p (g t w) -> p t g w", t=PACK, g=BLOCKS),
        )
        v_codes = [gather_words(0)]
        nc.scalar.copy(
            wg_sc[:].bitcast(U32).rearrange("p (t g w) -> p t g w", t=PACK, g=BLOCKS),
            wg_plane[:].bitcast(U32).rearrange("p (g t w) -> p t g w", t=PACK, g=BLOCKS),
        )
        v_codes.append(gather_words(1))

        def picked_gate(t, tag):
            gw = keep.tile([P, J], F32, name="gw", tag=tag, align_bytes=64)
            nc.vector.tensor_tensor(gw[:], gates[t][:].indirect(offsets[:]), wgo_sb[:], MULT)
            return gw

        gws = {SLOT_ORDER[0]: picked_gate(SLOT_ORDER[0], "gw0")}

        wu_bf = keep.tile([P, PACK * R], BF16, name="wu_bf", align_bytes=64)
        wu_dealt = wu_bf[:].rearrange("p (t g i j) -> p t g i j", t=PACK, g=BLOCKS, j=PACK)
        for h, wu_raw in enumerate(wu_halves):
            nc.scalar.copy(
                wu_dealt[:, :, WU_EDGES[h] : WU_EDGES[h + 1]],
                wu_raw[:].rearrange("p j (g t i) -> p t g i j", t=PACK, i=RUN),
            )
        wu_codes = keep.tile([P, R], U32, name="wu_codes", align_bytes=64)
        wu_sc = keep.tile([P, R], U8, name="wu_sc", align_bytes=64)
        nc.vector.quantize_mx(wu_codes[:].bitcast(FP8X4), wu_sc[:], wu_bf[:])

        def product(n, bank, w_codes, w_dtype, width, w_sc):
            acc = psum.tile([P, PACK, CHUNK], F32, name="acc", tag=bank)
            g = max(i for i, lo in enumerate(WORD_EDGES[:-1]) if lo <= n * CHUNK)
            piece = v_codes[g]
            first = n * CHUNK - WORD_EDGES[g]
            for t in range(PACK):
                nc.tensor.matmul_mx(
                    acc[:, t, :],
                    lhsT=w_codes[:, width * t : width * (t + 1)].bitcast(w_dtype),
                    lhsT_scale=w_sc[:, P * t : P * (t + 1)],
                    rhs=piece[:, first : first + CHUNK].bitcast(FP8X4),
                    rhs_scale=v_sc[:, n * CHUNK : (n + 1) * CHUNK],
                    start=True,
                    stop=True,
                )
            return acc

        gws[SLOT_ORDER[1]] = picked_gate(SLOT_ORDER[1], "gw1")
        second_page = keep.tile([P, T], F32, name="second_page", tag="wu_bf", align_bytes=64)
        nc.gpsimd.memset(second_page[:], 0.0)
        pages.append(second_page)
        early = WORD_EDGES[1] // CHUNK
        first_acts = keep.tile([P, early, CHUNK, PACK], F32, name="first_acts", align_bytes=64)
        later_acts = keep.tile([P, J // CHUNK - early, CHUNK, PACK], F32, name="later_acts", tag="wu_hi", align_bytes=64)
        acts = [first_acts[:, n] for n in range(early)] + [later_acts[:, n] for n in range(J // CHUNK - early)]

        def gelu_chunk(n):
            ga = product(n, f"bank{n}", wg_codes[:].bitcast(U8), FP4X4, 2 * P, wg_sc)
            nc.scalar.activation(acts[n], ga[:].rearrange("p t j -> p j t"), GELU)

        h_parts = [
            keep.tile([P, (hi - lo) * CHUNK, PACK], BF16, name="h_bf", tag=f"gate{SLOT_ORDER[1]}" if lo == 0 else f"h_bf{lo}", align_bytes=64)
            for lo, hi in zip(H_EDGES, H_EDGES[1:])
        ]

        def h_chunk(n, bank):
            g = max(i for i, lo in enumerate(H_EDGES[:-1]) if lo <= n)
            dst = h_parts[g][:, (n - H_EDGES[g]) * CHUNK : (n - H_EDGES[g] + 1) * CHUNK, :]
            ub = product(n, f"bank{bank}", wu_codes, FP8X4, P, wu_sc)
            if n >= GPSIMD_CHUNKS:
                nc.vector.tensor_tensor(dst, ub[:].rearrange("p t j -> p j t"), acts[n], MULT)
            else:
                ub_sb = keep.tile([P, CHUNK, PACK], F32, name="ub_sb", tag=f"ub_sb{n}", align_bytes=64)
                nc.scalar.copy(ub_sb[:], ub[:].rearrange("p t j -> p j t"))
                nc.gpsimd.tensor_tensor(dst, ub_sb[:], acts[n], MULT)

        for n in range(J // CHUNK):
            gelu_chunk(n)
            if n >= J // CHUNK - 1 - GPSIMD_CHUNKS and n < J // CHUNK - 1:
                h_chunk(n - 5, n - 5)
        for n in range(GPSIMD_CHUNKS, J // CHUNK):
            h_chunk(n, n)

        h_sc = keep.tile([P, J], U8, name="h_sc", align_bytes=64)
        h_codes = keep.tile([P, J], U32, name="h_codes", align_bytes=64)
        wd_codes = keep.tile([P, N], U32, name="wd_codes", align_bytes=64)
        wd_sc = keep.tile([P, N], U8, name="wd_sc", align_bytes=64)

        wd_bf = keep.tile([P, PACK * N], BF16, name="wd_bf", align_bytes=64)
        nc.scalar.copy(
            wd_bf[:].rearrange("p (t m s) -> p m s t", t=PACK, s=PACK),
            wd_raw[:].rearrange("p s (m t) -> p m s t", t=PACK),
        )
        nc.vector.quantize_mx(wd_codes[:].bitcast(FP8X4), wd_sc[:], wd_bf[:])
        for lo, hi, h_bf in zip(H_EDGES, H_EDGES[1:], h_parts):
            cols = slice(lo * CHUNK, hi * CHUNK)
            nc.vector.quantize_mx(h_codes[:, cols].bitcast(FP8X4), h_sc[:, cols], h_bf[:].rearrange("p j t -> p (j t)"))

        gws[SLOT_ORDER[2]] = picked_gate(SLOT_ORDER[2], "h_bf2")

        banks = [f"bank{b}" for b in range(8)]
        ys = {}
        for i, t in enumerate(SLOT_ORDER):
            ys[t] = keep.tile([P, J], F32, name=f"y{t}")
            for h in range(halves):
                y_ps = psum.tile([P, HALF], F32, name="y_ps", tag=banks[halves * i + h])
                nc.tensor.matmul_mx(
                    y_ps[:],
                    lhsT=wd_codes[:, P * t : P * (t + 1)].bitcast(FP8X4),
                    lhsT_scale=wd_sc[:, P * t : P * (t + 1)],
                    rhs=h_codes[:, h * HALF : (h + 1) * HALF].bitcast(FP8X4),
                    rhs_scale=h_sc[:, h * HALF : (h + 1) * HALF],
                    start=True,
                    stop=True,
                )
                nc.scalar.copy(ys[t][:, h * HALF : (h + 1) * HALF], y_ps[:])

        out_bf = keep.tile([P, T, PACK], BF16, name="out_bf", align_bytes=64)
        out_rows = out_0.rearrange("(p t) c -> t p c", t=PACK)
        spans = [slice(lo, hi) for lo, hi in zip(SPAN_EDGES, SPAN_EDGES[1:])]
        for i, t in enumerate(SLOT_ORDER):
            if i == PACK - 2:
                gws[SLOT_ORDER[-1]] = picked_gate(SLOT_ORDER[-1], "gw0")
            page = pages[i % 2]
            nc.vector.tensor_tensor(page[:].indirect(offsets[:]), ys[t][:], gws[t][:], MULT)
            nc.sync.dma_start(out_rows[t], page[:])
            if i < PACK - 1:
                nc.scalar.copy(out_bf[:, :, t], page[:])
            else:
                for a, s in enumerate(spans):
                    if a < VECTOR_SPANS:
                        nc.vector.tensor_copy(out_bf[:, s, t], page[:, s])
                    else:
                        nc.scalar.copy(out_bf[:, s, t], page[:, s])

        out_sc = keep.tile([P, QUARTER], U8, name="out_sc", align_bytes=64)
        out_codes = keep.tile([P, T], I32, name="out_codes", align_bytes=64)
        out_words = out_1[0].rearrange("p t i -> p (t i)").bitcast(I32)
        for s in spans:
            for lo in range(s.start, s.stop, PIECE):
                cols = slice(lo, lo + PIECE)
                plane = out_sc[4 * (lo // QUARTER) :, lo % QUARTER : lo % QUARTER + PIECE]
                nc.vector.quantize_mx(out_codes[:, cols].bitcast(FP8X4), plane, out_bf[:, cols, :].rearrange("p c t -> p (c t)"))
            nc.sync.dma_start(out_words[:, s], out_codes[:, s])
        for q in range(4):
            queue = nc.scalar if q % 2 == 0 else nc.sync
            queue.dma_start(
                out_2[0, 4 * q : 4 * q + 4, :].bitcast(I32).rearrange("r (k c) -> k r c", k=4),
                out_sc[32 * q : 32 * q + 16, :].bitcast(I32),
            )
